import numpy as np, ml_dtypes
CORES = [36,164,52,180,100,228,116,244]
N = 8
BF = ml_dtypes.bfloat16
W, I, S, JU, RO = 2560, 1024, 4, 8, 2
def pick(a, ix):
    return np.take_along_axis(a, ix, 2) if a.ndim == 3 else np.take_along_axis(a, ix[:, :, None, :], 3)
def walk(u, par, side, heads):
    w = heads; c = heads; acc = np.zeros((N, 8, 16, I), np.int64)
    for _ in range(S):
        v = pick(u, w); up = np.add.reduce((v >= 4).astype(np.int64), axis=2) >= 9
        acc = acc + np.where(up[:, :, None, :], v, 0)
        sd = pick(side, c); w = np.where(up, pick(par, w), sd); c = np.where(up, c, sd)
    return acc
def forest(rng, alike, noise, ex):
    par = np.zeros((N, 8, W), np.int64); side = np.zeros((N, 8, W), np.int64); itm = np.zeros((N, 8, W), np.int64); bit = np.zeros((N, 8, W), np.int64); heads = np.zeros((N, 8, I), np.int64)
    pop = [rng.permutation(I) for g in range(8)]; n = np.arange(W); m = np.arange(W - 1)
    for q in range(N):
        for g in range(8):
            it = pop[g][np.minimum((I * rng.random(W) ** ex).astype(np.int64), I - 1)]; itm[q, g] = it
            o = np.argsort(it[1:], kind="stable") + 1; k = it[o]
            new = np.concatenate([np.array([True]), k[1:] != k[:-1]])
            side[q, g, o[:-1]] = np.where(new[1:], 0, o[1:]); heads[q, g, k[new]] = o[new]
            base = np.maximum(np.minimum((n * rng.random(W) ** 0.4).astype(np.int64), n - 1), 0)
            run = np.maximum.accumulate(np.where(new | (rng.random(W - 1) >= alike), m, 0))
            par[q, g, o] = base[o[run]]
            bit[q, g, o] = (m + (rng.random(W - 1) < noise)) & 1
    return par, side, itm, bit, heads
def counts(rng, e):
    lev = rng.random((N, 8, 1, W)) ** e
    u = np.where(rng.random((N, 8, 16, W)) < lev, rng.integers(4, 16, (N, 8, 16, W)), rng.integers(0, 4, (N, 8, 16, W)))
    u[..., 0] = 0
    return u
def level(u, par, side, heads, share):
    s = np.sort(np.add.reduce(walk(u, par, side, heads), axis=0), axis=2)
    j = np.minimum((I * share).astype(np.int64), I - 1)
    return np.clip(s[np.arange(8)[:, None], np.arange(16)[None, :], j[:, None]], 1, 1024)
def pack(u, par, side, itm, bit, heads, th):
    return {"cnt": np.ascontiguousarray(u.reshape(N, 128, W)).astype(np.float32).astype(BF), "par": par.astype(np.int32), "side": side.astype(np.int32), "itm": itm.astype(np.int32),
            "bit": bit.astype(np.int32), "heads": heads.astype(np.int32), "th": np.repeat(th.reshape(1, 128, 1), N, axis=0).astype(np.int32)}
def setup_inputs(rng):
    par, side, itm, bit, heads = forest(rng, 0.5, 0.25, 2.0); u = counts(rng, 0.5)
    return pack(u, par, side, itm, bit, heads, level(u, par, side, heads, 0.35 + 0.4 * rng.random(8)))
def setup_inputs_ties(rng):
    par, side, itm, bit, heads = forest(rng, 0.5, 0.25, 2.0)
    r = np.argsort(rng.random((N, 8, 16, W)), axis=2); m = 8 + (rng.random((N, 8, 1, W)) < 0.7)
    u = np.where(r < m, np.where(rng.random(r.shape) < 0.8, 4, rng.integers(4, 16, r.shape)), 3); u[..., 0] = 0
    tot = np.add.reduce(walk(u, par, side, heads), axis=0)
    i0 = np.argsort(np.min(tot, axis=1), axis=1, kind="stable")[:, I // 2]
    x = np.stack([tot[g, :, i0[g]] for g in range(8)]); k = np.argsort(rng.random((8, 16)), axis=1)
    th = np.where(k < 8 + (np.arange(8)[:, None] & 1), x, x + 1)
    return pack(u, par, side, itm, bit, heads, np.clip(th, 1, 1024))
def setup_inputs_deep(rng):
    par, side, itm, bit, heads = forest(rng, 0.5, 0.25, 2.0); u = counts(rng, 0.5); n = np.arange(W)
    par[:, 0::2] = np.maximum(n - 1, 0); par[:, 1::2] = np.maximum(n - 1 - rng.integers(0, 3, (N, 4, W)), 0)
    u = np.where(rng.random((N, 8, 1, W)) < 0.15, 15, u); u[..., 0] = 0
    th = level(u, par, side, heads, np.array([0.8, 0.9, 0.7, 0.5, 0.5, 0.5, 0.95, 0.6]))
    th[3] = 1024; th[4] = 1
    return pack(u, par, side, itm, bit, heads, th)
def one_chain(rng, par, side, itm, bit, heads, u):
    for q in range(N):
        for g in range(4):
            o = np.concatenate([np.array([W - 1]), rng.permutation(W - 2) + 1]); top = o[1]
            side[q, g] = 0; side[q, g, o[:-1]] = o[1:]
            if g == 1: side[q, g, o[1::2]] = 0
            bit[q, g, o] = (np.arange(W - 1) + (g == 1)) & 1
            par[q, g] = top; par[q, g, 0] = 0
            itm[q, g] = rng.integers(0, I, W); itm[q, g, top] = 0
            heads[q, g] = rng.integers(1, W, I); heads[q, g, 0] = top
            u[q, g] = rng.integers(4, 16, (16, W)); u[q, g, :, top] = rng.integers(12, 16, 16); u[q, g, :, 0] = 0
def setup_inputs_merge(rng):
    par, side, itm, bit, heads = forest(rng, 0.9, 0.5, 3.0); u = counts(rng, 0.4)
    one_chain(rng, par, side, itm, bit, heads, u)
    th = level(u, par, side, heads, 0.03 + 0.17 * rng.random(8))
    tot = np.add.reduce(walk(u, par, side, heads), axis=0)
    th[:2] = np.min(tot[:2], axis=2)
    th[2] = np.sort(tot[2], axis=1)[:, I // 2] | 1
    i0 = np.argsort(np.add.reduce(tot[3], axis=0), kind="stable")[I // 2]; k = np.argsort(rng.random(16))
    th[3] = np.where(k < 9, tot[3, :, i0], tot[3, :, i0] + 1)
    return pack(u, par, side, itm, bit, heads, th)
def setup_inputs_wild(rng):
    par = rng.integers(0, W, (N, 8, W)); itm = rng.integers(0, I, (N, 8, W)); bit = rng.integers(0, 2, (N, 8, W)); side = np.zeros((N, 8, W), np.int64)
    par[..., 1] = W - 1; zz = np.zeros((N, 8), np.int64)
    for q in range(N):
        for g in range(8):
            o = rng.permutation(W - 1) + 1; x, y, z, rest = o[:32], o[32:64], o[64], o[65:]
            a, b = rng.permutation(rest), rng.permutation(rest); h = W - W // 5
            side[q, g, a[:h]] = b[:h]; side[q, g, x] = y; side[q, g, y] = x; side[q, g, z] = z; zz[q, g] = z; bit[q, g, x] = 0; bit[q, g, y] = 1
            sel = np.nonzero((side[q, g] > 0) & (rng.random(W) < 0.6))[0]; p = par[q, g].copy(); p[side[q, g, sel]] = par[q, g, sel]; p[y] = p[x]; p[z] = 0; par[q, g] = p
    par[..., 0] = 0
    heads = np.where(rng.random((N, 8, I)) < 0.3, rng.choice(np.array([0, 1, W - 1]), (N, 8, I)), rng.integers(0, W, (N, 8, I)))
    heads[:, 0] = rng.choice(np.array([1, W - 1, W // 2, 5]), (N, I))
    heads[:, :, 3] = zz
    u = counts(rng, 0.5); u[np.arange(N)[:, None], np.arange(8)[None, :], :, zz] = 15
    return pack(u, par, side, itm, bit, heads, level(u, par, side, heads, 0.3 + 0.3 * rng.random(8)))
def setup_inputs_spread(rng):
    par, side, itm, bit, heads = forest(rng, rng.random(), 0.3, 4.0)
    u = np.minimum((16 * rng.random((N, 8, 16, W)) ** np.exp2(rng.integers(-3, 3, (N, 8, 1, W)))).astype(np.int64), 15)
    u = np.where(rng.random((N, 8, 1, W)) < 0.0625, 0, u); u[..., 0] = 0
    return pack(u, par, side, itm, bit, heads, level(u, par, side, heads, rng.permutation(np.array([0.02, 0.15, 0.3, 0.45, 0.55, 0.7, 0.85, 0.97]))))
def check_inputs(d):
    bad = []
    for k, lo, hi in (("par", 0, W - 1), ("side", 0, W - 1), ("itm", 0, I - 1), ("bit", 0, 1), ("heads", 0, W - 1), ("th", 1, 1024)):
        if np.min(d[k]) < lo or np.max(d[k]) > hi: bad.append("range of " + k)
    c = d["cnt"].astype(np.float32)
    if not np.all((c >= 0) & (c <= 15) & (c == np.floor(c))): bad.append("cnt: whole numbers from 0 to 15")
    if np.any(c[:, :, 0] != 0): bad.append("cnt of node 0")
    for k in ("par", "side"):
        if np.any(d[k][:, :, 0] != 0): bad.append(k + " of node 0")
    s = np.sort(d["side"], axis=2)
    if np.any((s[:, :, 1:] == s[:, :, :-1]) & (s[:, :, 1:] != 0)): bad.append("side: numbers other than 0 differ")
    if np.any(d["th"] != d["th"][:1]): bad.append("th alike on all ranks")
    return bad
def reference(cnt, par, side, itm, bit, heads, th):
    u = cnt.astype(np.float32).astype(np.int64).reshape(N, 8, 16, W); pa = par.astype(np.int64); sd = side.astype(np.int64)
    it = itm.astype(np.int64); b = bit.astype(np.int64); hd = heads.astype(np.int64); lim = th[0].astype(np.int64).reshape(8, 16, 1)
    node = np.broadcast_to(np.arange(W), (N, 8, W)); own = []
    for t in range(RO):
        tot = np.add.reduce(walk(u, pa, sd, hd), axis=0)
        own.append(np.stack([tot[:, :, r * (I // N):(r + 1) * (I // N)].reshape(128, I // N) for r in range(N)]))
        kept = np.add.reduce((tot >= lim).astype(np.int64), axis=1) >= 9
        kn = pick(np.broadcast_to(kept[None], (N, 8, I)), it); kn[:, :, 0] = True
        jump = np.where(kn, node, pa); p1 = pa
        for _ in range(JU): p1 = pick(jump, p1)
        u1 = np.where(pick(kn, pa)[:, :, None, :], u, np.minimum(15, u + pick(u, pa)))
        ab = kn & (sd != 0) & (p1 == pick(p1, sd)) & (b == t % 2) & (pick(b, sd) == 1 - t % 2)
        u = np.where(ab[:, :, None, :], np.minimum(15, u1 + pick(u1, sd)), u1)
        rep = np.array(node); a, g, n = np.nonzero(ab); rep[a, g, sd[a, g, n]] = n
        sd = np.where(ab, pick(sd, sd), np.where(rep != node, 0, sd))
        pa = pick(rep, p1)
    return {"ya": np.concatenate(own, axis=2).astype(np.float32), "yc": np.ascontiguousarray(u.reshape(N, 128, W)).astype(np.float32).astype(BF), "yp": pa.astype(np.float32)}

@@ -1,0 +1,644 @@
+from concourse.bass import DstId, RemoteDMATransfer
+from concourse.mybir import AluOpType, ActivationFunctionType
+
+NW, NI, NC = 2560, 1024, 160
+H = NW // 2
+R_N, R_PAR, R_PU, R_SIDE, R_ITM, R_DS, R_ONE, R_UP, R_BIT, R_NZ = 0, 2, 4, 6, 8, 10, 12, 13, 14, 15
+
+
+def pair(r, w=1.0):
+    return {r: w, r + 1: w}
+
+
+def join(*ds):
+    o = {}
+    for d in ds:
+        o.update(d)
+    return o
+
+
+SIDE = join(pair(R_SIDE), pair(R_DS))
+ZS = [
+    ("all", None),
+    ("head", pair(R_DS)),
+    ("side", SIDE),
+    ("x", join(SIDE, {R_UP: 4096.0})),
+    ("lin", join(pair(R_PU), SIDE, {R_UP: 2560.0})),
+    ("par", pair(R_PAR)),
+    ("lin0", join(pair(R_PU), SIDE)),
+    ("bit", {R_BIT: 1.0}),
+    ("i2b", join(pair(R_ITM), {R_BIT: 2048.0})),
+    ("bm", {R_BIT: -2048.0}),
+    ("itm", pair(R_ITM)),
+    ("sg0", {R_BIT: -1024.0, R_NZ: -1024.0}),
+    ("a0", join(pair(R_ITM), {R_BIT: 1024.0, R_ONE: -1024.0})),
+    ("n", pair(R_N)),
+    ("j", join(pair(0), pair(2))),
+    ("r", join(pair(4), pair(6))),
+    ("kp", {R_ONE: -2560.0}),
+    ("drop", {2: 4096.0}),
+    ("i2bn", join(pair(R_ITM), {R_BIT: -2048.0})),
+    ("sg1", {R_BIT: 1024.0, R_NZ: -1024.0}),
+    ("a1", join(pair(R_ITM), {R_BIT: -1024.0})),
+    ("bp", {R_BIT: 2048.0}),
+]
+ZI = {z[0]: k for k, z in enumerate(ZS)}
+ZE = 7
+ZM = 11
+ZW = 144
+
+SCRATCH = {}
+for _n in ("Ub", "A", "B", "C", "KA", "GE", "Y", "UM", "SG", "X", "Ud"):
+    SCRATCH[_n] = ("sbuf", [128, NW], "bfloat16")
+for _n in ("W", "SW", "Ua", "Uc"):
+    SCRATCH[_n] = ("sbuf", [128, 2 * NW], "bfloat16")
+for _n in ("F0", "F1", "G0", "G1", "G2", "S", "ACC0", "ACC1", "LAND0", "LAND1"):
+    SCRATCH[_n] = ("sbuf", [128, NI], "bfloat16")
+for _n in ("KW0", "KW1"):
+    SCRATCH[_n] = ("sbuf", [128, NI + 16], "bfloat16")
+SCRATCH["ZZ"] = ("sbuf", [128, len(ZS) * ZW], "bfloat16")
+for _n in ("IDb", "BO", "s1", "s2", "c15"):
+    SCRATCH[_n] = ("sbuf", [128, 128], "bfloat16")
+for _n in ("IDf", "tot0", "tot1"):
+    SCRATCH[_n] = ("sbuf", [128, 128], "float32")
+O_SIDE, O_HEAD, O_PAR, O_ITM, O_N, O_BIT, O_END = 0, 160, 224, 384, 544, 704, 864
+SCRATCH["LI"] = ("sbuf", [128, O_END], "int32")
+SCRATCH["LF"] = ("sbuf", [128, O_END], "float32")
+SCRATCH["LH"] = ("sbuf", [128, O_END], "bfloat16")
+SCRATCH["LL"] = ("sbuf", [128, O_END], "bfloat16")
+for _n in ("nI", "n2560", "sideI", "bitI", "predI", "sA0", "sA1", "t1", "t2", "t3", "P8I", "P8B", "mI",
+           "D0", "eB", "nbB", "ypB", "kaT", "bpI"):
+    SCRATCH[_n] = ("sbuf", [128, NC], "float32")
+for _n in ("upB", "puH", "puL", "dH", "dL", "sH", "sL", "pH", "pL", "DH", "DL", "mB", "SH", "SL", "zB"):
+    SCRATCH[_n] = ("sbuf", [128, NC], "bfloat16")
+for _n in ("par16", "side16", "ip16", "sc16", "ka16", "pt16", "pred16", "j1", "j2", "j4l", "pe16", "p816", "se16"):
+    SCRATCH[_n] = ("sbuf", [128, NC], "uint16")
+for _n in ("hd16", "ix1", "ix2", "w1", "w2", "w3"):
+    SCRATCH[_n] = ("sbuf", [128, 64], "uint16")
+for _n in ("k0", "k1", "k2", "wa", "wb", "wu"):
+    SCRATCH[_n] = ("sbuf", [128, 64], "float32")
+for _n in ("thI", "pI", "fI", "fH"):
+    SCRATCH[_n] = ("sbuf", [128, 4], "int32")
+for _n in ("thb", "fF", "f160", "dcol", "scol"):
+    SCRATCH[_n] = ("sbuf", [128, 4], "float32")
+SCRATCH["z8"] = ("sbuf", [128, 8], "bfloat16")
+for _k in range(8):
+    SCRATCH["p%d" % _k] = ("psum", [128, 512], "float32")
+
+ENG = ["pe", "dve", "act", "pool"]
+DMAG = ["ld", "ldu0", "ldu1", "ldth", "hd0", "wa0", "fw0", "fx0", "fw1", "fx1", "rp0", "rp1", "sd1", "pr1", "vv0", "xr0",
+        "xr1", "ya0", "ya1", "yc0", "yc1", "yc2", "yc3", "yp0", "vv1"] + \
+    ["ud%d_%d" % (_t, _j) for _t in range(2) for _j in range(4)]
+SEMAPHORES = ["e_" + _e for _e in ENG] + ["d_" + _d for _d in DMAG] + ["sent"] + \
+    ["rs%d_%d" % (_t, _m) for _t in range(2) for _m in range(4)] + ["ag0", "ag1"]
+
+ADD, SUB, MUL, MAX, MIN = AluOpType.add, AluOpType.subtract, AluOpType.mult, AluOpType.max, AluOpType.min
+GE_, EQ, NE = AluOpType.is_ge, AluOpType.is_equal, AluOpType.not_equal
+AND = AluOpType.bitwise_and
+AF = ActivationFunctionType
+SPLIT = 672
+PSPLIT = 640
+CUT = (768, 640, 544)
+TAIL = [(640 * _j, 640 * (_j + 1)) for _j in range(4)]
+
+
+def rank_program(g, core, T, topo):
+    rank = T.rank_of(core)
+    if rank is None:
+        return
+    N = len(T.cores)
+    Q = {"pe": g.tensor, "dve": g.vector, "act": g.scalar, "pool": g, "sp": g.sync}
+    ops = []
+    sent = [0]
+
+    def reg(x):
+        if isinstance(x, str):
+            return (x, 0, 1 << 20, None)
+        return (x[0], x[1], x[2], x[3] if len(x) > 3 else None)
+
+    def op(eng, fn, r=(), w=(), grp=None, ext=(), inc=True):
+        ops.append({"e": eng, "fn": fn, "r": [reg(x) for x in r], "w": [reg(x) for x in w], "grp": grp, "ext": list(ext),
+                    "inc": inc})
+
+    def ap(x):
+        x = reg(x)
+        if x[2] == 1 << 20:
+            return T[x[0]][:]
+        return T[x[0]][:, x[1]:x[2]]
+
+    def ts(o, i, s1, op0, s2=None, op1=None):
+        a1 = T[s1][:, 0:1] if isinstance(s1, str) else s1
+        rd = [i] + ([s1] if isinstance(s1, str) else [])
+        if op1 is None:
+            op("dve", lambda: g.vector.tensor_scalar(ap(o), ap(i), a1, None, op0), rd, [o])
+        else:
+            op("dve", lambda: g.vector.tensor_scalar(ap(o), ap(i), a1, s2, op0, op1), rd, [o])
+
+    def tt(o, a, b, alu):
+        op("dve", lambda: g.vector.tensor_tensor(ap(o), ap(a), ap(b), alu), [a, b], [o])
+
+    def cp(o, i):
+        op("dve", lambda: g.vector.tensor_copy(ap(o), ap(i)), [i], [o])
+
+    def ms(o, v):
+        op("dve", lambda: g.vector.memset(ap(o), v), [], [o])
+
+    def act(o, i, func=AF.Identity, bias=0.0, scale=1.0):
+        b = T[bias][:, 0:1] if isinstance(bias, str) else bias
+        s = T[scale][:, 0:1] if isinstance(scale, str) else scale
+        rd = [i] + [x for x in (bias, scale) if isinstance(x, str)]
+        op("act", lambda: g.scalar.activation(ap(o), ap(i), func, bias=b, scale=s), rd, [o])
+
+    def gather(eng, o, win, lst, a, b, in1=None, alu=None, ext=(), shift=0):
+        l = (lst, a // 16, b // 16)
+        out = (o, shift + a, shift + b)
+        rd = [win, l] + ([(in1, a, b)] if in1 else [])
+        if eng == "act":
+            fn = lambda: g.scalar.activation(ap(out), ap(win).indirect(ap(l)), AF.Copy)
+        elif in1:
+            fn = lambda: g.vector.tensor_tensor(ap(out), ap(win).indirect(ap(l)), T[in1][:, a:b], alu)
+        else:
+            fn = lambda: g.vector.tensor_copy(ap(out), ap(win).indirect(ap(l)))
+        op(eng, fn, rd, [out], ext=ext)
+
+    def sel(z, i):
+        z0 = ZI[z] * ZW
+        return T.ZZ[:, z0 + 16 - i:z0 + ZW - i]
+
+    def zreg(z):
+        return ("ZZ", ZI[z] * ZW, (ZI[z] + 1) * ZW)
+
+    def extI(bank, src, z, a=0, b=NW, start=True, stop=True, o=None):
+        o0 = a // 16 if o is None else o
+
+        def fn():
+            for i in range(16):
+                ins = g.tensor.matmul(T[bank][:, o0:o0 + (b - a) // 16], sel(z, i), T[src][:, a + i:b:16],
+                                      start and i == 0, stop and i == 15)
+            return ins
+        op("pe", fn, [(src, a, b), zreg(z)], [bank])
+
+    def extB(bank, src, z, i0=0, i1=16, start=True, stop=True):
+        def fn():
+            for i in range(i0, i1):
+                ins = g.tensor.matmul(T[bank][:, 0:NC], sel(z, i), T[src][:, NC * i:NC * (i + 1)],
+                                      start and i == i0, stop and i == i1 - 1)
+            return ins
+        op("pe", fn, [(src, NC * i0, NC * i1), zreg(z)], [bank])
+
+    def mm(o, lhs, rhs, start, stop, ext=()):
+        op("pe", lambda: g.tensor.matmul(ap(o), T[lhs][:], ap(rhs), start, stop), [lhs, rhs], [o], ext=ext)
+
+    def dma(q, grp, out, in_, r, w):
+        op(q, lambda: Q[q].dma_start(out, in_), r, w, grp=grp)
+
+    def row(q, grp, win, f, src, c0=0, n=NW):
+        dma(q, grp, T[win][f::16, c0:c0 + n], ap(src), [src], [(win, c0, c0 + n, f)])
+
+    def digits(hi, lo, v):
+        cp(hi, v)
+        tt(lo, v, hi, SUB)
+
+    def P(bank, n=NC, o=0):
+        return (bank, o, o + n)
+
+    def L(buf, o, n=NC):
+        return (buf, o, o + n)
+
+    def dst(r):
+        rid, pid = topo.addr(T.cores[r], core)
+        return DstId(rid=rid, pnc=pid)
+
+    def engs(r, part, parts):
+        e = topo.engines(core, T.cores[r])
+        k = len(e) // parts
+        return e[part * k:(part + 1) * k]
+
+    def bits(e):
+        return sum(1 << x for x in e)
+
+    def iota(o, pat, cm, small):
+        if small:
+            op("pool", lambda: g.iota(ap(o), pat, 0, cm, allow_small_or_imprecise_dtypes=True), [], [o])
+        else:
+            op("pool", lambda: g.iota(ap(o), pat, 0, cm), [], [o])
+
+    def asel(o, oap, i, iap, pat, cmp, fill, base, cm):
+        op("pool", lambda: g.affine_select(oap, iap, pat, cmp, fill, base, cm), [i], [o])
+
+    def make_z(k):
+        name, wts = ZS[k]
+        v = T.ZZ[:, k * ZW + 16:(k + 1) * ZW:16]
+        if wts is None:
+            asel("z8", T.z8[:], "IDb", T.IDb[:, 0:8], [[-16, 8]], GE_, 0.0, 0, 1)
+            asel(zreg(name), v, "z8", T.z8[:], [[16, 8]], GE_, 0.0, 15, -1)
+        else:
+            for f in sorted(wts):
+                asel(zreg(name), v, zreg(name), v, [[-16, 8]], NE, wts[f], -f, 1)
+
+    def zero(o, i):
+        act(o, i, AF.Identity, 0.0, 0.0)
+
+    for name, o, n in (("side", O_SIDE, NC), ("heads", O_HEAD, 64), ("par", O_PAR, NC), ("itm", O_ITM, NC), ("bit", O_BIT, NC)):
+        dma("sp", "ld", T.LI[:, o:o + n], T[name][:], [], [L("LI", o, n)])
+    dma("act", "ldu0", T.Ua[:, 0:H], T.cnt[:, 0:H], [], [("Ua", 0, H)])
+    dma("act", "ldu1", T.Ua[:, H:NW], T.cnt[:, H:NW], [], [("Ua", H, NW)])
+    iota(("pI", 0, 1), [[0, 1]], 1, False)
+    iota(L("LF", O_N), [[1, NC]], 0, True)
+    iota("nI", [[16, NC]], 0, True)
+    ms(("W", 0, 640), 1.0)
+    ms(("ZZ", 0, ZE * ZW), 0.0)
+    ms("IDb", 1.0)
+    ms("c15", 15.0)
+    act(("W", 640, 1280), ("W", 0, 640), AF.Copy)
+    act(("W", 1280, NW), ("W", 0, 1280), AF.Copy)
+    make_z(0)
+    asel("BO", T.BO[:], "c15", T.c15[:], [[-16, 8], [0, 16]], GE_, 0.0, 0, 1)
+    asel("BO", T.BO[:], "BO", T.BO[:], [[16, 8], [0, 16]], GE_, 0.0, 15, -1)
+    make_z(1)
+    asel("IDb", T.IDb[:], "IDb", T.IDb[:], [[-1, 128]], EQ, 0.0, 0, 1)
+    for k in range(2, ZE):
+        make_z(k)
+    iota(("ZZ", ZE * ZW, len(ZS) * ZW), [[0, (len(ZS) - ZE) * ZW]], 0, True)
+    op("pool", lambda: g.dma_start(T.thI[:, 0:1], T.th[:], allow_slow_non_contiguous=True), [], [("thI", 0, 1)], grp="ldth")
+    for k in range(ZE, ZM):
+        make_z(k)
+    ts(("fI", 0, 1), ("pI", 0, 1), 15, AND)
+    cp(("fF", 0, 1), ("fI", 0, 1))
+    ts(("fH", 0, 1), ("pI", 0, 1), 10, AND)
+    ts(("f160", 0, 1), ("fF", 0, 1), 160.0, MUL)
+    ts(("dcol", 0, 1), ("fH", 0, 1), 2.0, EQ)
+    ts(L("LF", O_N), L("LF", O_N), "f160", ADD)
+    ts(("scol", 0, 1), ("dcol", 0, 1), -2.0, MUL, 1.0, ADD)
+    ms("zB", 0.0)
+    ts("nI", "nI", "fF", ADD)
+    ts("n2560", "nI", float(NW), ADD)
+    cp(("LF", 0, O_N), ("LI", 0, O_N))
+    cp(L("LF", O_BIT), L("LI", O_BIT))
+    ts(("W", 0, 1), ("fF", 0, 1), float(R_NZ), NE)
+    act("LH", "LF", AF.Copy)
+    row("sp", "wa0", "W", R_DS, "zB")
+    row("sp", "wa0", "W", R_DS + 1, "zB")
+    zero(("SW", 0, H), ("Ua", 0, H))
+
+    def ge4(U, a, b, first, eng="dve"):
+        if eng == "dve":
+            ts(("GE", a, b), (U, a, b), 4.0, GE_, 0.5, SUB)
+        else:
+            act(("GE", a, b), (U, a, b), AF.Sign, -3.5)
+        extB("p0", "GE", "all", a // NC, b // NC, first, b == NW)
+
+    def prep(t, U):
+        if t == 0:
+            ge4(U, 0, H, True)
+            ge4(U, H, NW, False)
+            tt(("LL", 0, O_BIT), ("LF", 0, O_BIT), ("LH", 0, O_BIT), SUB)
+            row("sp", "wa0", "W", R_BIT, L("LH", O_BIT))
+            for f, o in ((R_SIDE, O_SIDE), (R_PAR, O_PAR), (R_ITM, O_ITM), (R_N, O_N)):
+                row("sp", "wa0", "W", f, L("LH", o))
+            row("sp", "hd0", "SW", R_DS, L("LH", O_HEAD, 64), 0, NI)
+            row("sp", "hd0", "SW", R_DS + 1, L("LL", O_HEAD, 64), 0, NI)
+            for f, o in ((R_SIDE, O_SIDE), (R_PAR, O_PAR), (R_ITM, O_ITM), (R_N, O_N)):
+                row("sp", "wa0", "W", f + 1, L("LL", o))
+            zero(("W", NW, NW + H), ("Ua", 0, H))
+            ph, pl = L("LH", O_PAR), L("LL", O_PAR)
+        else:
+            ph, pl = "pH", "pL"
+        ts("upB", P("p0"), 0.5, GE_)
+        row("act", "fw%d" % t, "W", R_UP, "upB")
+        tt("puH", ph, "upB", MUL)
+        row("sp", "fw%d" % t, "W", R_PU, "puH")
+        tt("puL", pl, "upB", MUL)
+        row("sp", "fw%d" % t, "W", R_PU + 1, "puL")
+        if t == 0:
+            zero(("W", NW + H, 2 * NW), ("Ua", H, NW))
+            zero(("SW", H, NW), ("Ua", H, NW))
+        for f, s in ((R_UP, "upB"), (R_PU, "puH"), (R_PU + 1, "puL")):
+            row("sp", "fx%d" % t, "W", f, s, NW)
+        for c in range(5):
+            b = "p%d" % (4 + c % 2)
+            mm(b, "BO", ("GE", 512 * c, 512 * (c + 1)), True, True)
+            tt(("Y", 512 * c, 512 * (c + 1)), b, (U, 512 * c, 512 * (c + 1)), MIN)
+            if t == 0 and c == 3:
+                extI("p1", "SW", "head", 0, NI)
+                cp("hd16", P("p1", 64))
+        if t == 0:
+            cp("IDf", "IDb")
+            extI("p2", "W", "side")
+
+    def walks(t):
+        acc = "ACC%d" % t
+        gather("act", "F0", ("W", 0, NW), "hd16", 0, NI)
+        for h in range(2):
+            ts(("UM", h * H, (h + 1) * H), ("Y", h * H, (h + 1) * H), 0.0, MAX, 15.0, MIN)
+        lists = ["hd16", "w1", "w2", "w3"]
+        for s in range(3):
+            k, F = "k%d" % s, "F%d" % (s % 2)
+            for bank, z in (("p0", "x"), ("p1", "lin" if s < 2 else "lin0")):
+                if s > 0:
+                    mm(P(bank, 64), "IDf", "k%d" % (s - 1), True, False)
+                extI(bank, F, z, 0, NI, s == 0, True)
+            if s == 0 and t == 0:
+                extI("p3", "W", "par")
+            gather("act", "G%d" % s, "UM", lists[s], 0, CUT[s])
+            gather("dve", "G%d" % s, "UM", lists[s], CUT[s], NI)
+            ts(k, P("p0", 64), -4096.0, ADD, 0.0, MAX)
+            if s < 2:
+                ts("wu", P("p0", 64), 4096.0, GE_, float(NW), MUL)
+            tt("wa", P("p1", 64), k, SUB)
+            cp("ix%d" % (s + 1) if s < 2 else "w3", "wa")
+            for h in range(2):
+                mm("p%d" % (6 + h), "IDb", ("G%d" % s, 512 * h, 512 * (h + 1)), s == 0, s == 2)
+            if s < 2:
+                F = "F%d" % ((s + 1) % 2)
+                tt("wb", "wa", "wu", SUB)
+                gather("act", F, "W", "ix%d" % (s + 1), 0, 512)
+                gather("dve", F, "W", "ix%d" % (s + 1), 512, NI)
+                cp(lists[s + 1], "wb")
+        if t == 0:
+            cp("par16", P("p3"))
+        else:
+            cp("pred16", "predI")
+        order = [(rank // 2 + m) % 4 for m in (1, 2, 3, 0)]
+        for c in order:
+            act(("S", 256 * c, 256 * (c + 1)), ("p%d" % (6 + c // 2), 256 * (c % 2), 256 * (c % 2 + 1)), AF.Copy)
+        for m, c in enumerate(order):
+            gather("dve", acc, "UM", "w3", 256 * c, 256 * (c + 1), "S", ADD)
+            to = [r for r in (2 * c, 2 * c + 1) if r != rank]
+
+            def send(to=to, m=m):
+                tr = [RemoteDMATransfer(dst_ids=[dst(r)], dma_engine_mask=bits(engs(r, j, len(to))),
+                                        remote_sem=T.sem["rs%d_%d" % (t, m)], src=T[acc][:, 128 * r:128 * (r + 1)],
+                                        dst=T["LAND%d" % t][:, 128 * rank:128 * (rank + 1)]) for j, r in enumerate(to)]
+                return g.remote_dma_fused(tr, local_sem=T.sem.sent)
+            sent[0] += sum(len(engs(r, j, len(to))) for j, r in enumerate(to))
+            op("pool", send, [(acc, 256 * c, 256 * (c + 1))], [], inc=False)
+
+    def verdict(t):
+        acc, land, kw = "ACC%d" % t, "LAND%d" % t, "KW%d" % t
+        own = (128 * rank, 128 * (rank + 1))
+        mm(P("p4", 128), "IDb", (acc,) + own, True, False)
+        for m in range(4):
+            c = (rank // 2 - (m + 1)) % 4
+            frm = [r for r in (2 * c, 2 * c + 1) if r != rank]
+            cnt = sum(len(topo.engines(T.cores[r], core)) // len(frm) for r in frm)
+            for r in frm:
+                mm(P("p4", 128), "IDb", (land, 128 * r, 128 * (r + 1)), False, m == 3, ext=[("rs%d_%d" % (t, m), cnt)])
+        act("s1", P("p4", 128), AF.Sign, "thb")
+        mm(P("p5", 128), "BO", "s1", True, True)
+        act("s2", P("p5", 128), AF.Sign, -15.0)
+        act((kw,) + own, "s2", AF.Relu, 0.0, "scol")
+        oth = [(rank + d) % N for d in range(1, N)]
+
+        def send():
+            a = T[kw][:, own[0]:own[1]]
+            tr = RemoteDMATransfer(dst_ids=[dst(r) for r in oth], dma_engine_mask=bits(engs(oth[0], 0, 1)),
+                                   remote_sem=T.sem["ag%d" % t], srcs=[a], dsts=[a for r in oth])
+            return g.remote_dma_fused([tr], local_sem=T.sem.sent)
+        sent[0] += len(engs(oth[0], 0, 1))
+        op("pool", send, [(kw,) + own], [], inc=False)
+        act("tot%d" % t, P("p4", 128))
+        dma("sp", "ya%d" % t, T.ya[:, 128 * t:128 * (t + 1)], T["tot%d" % t][:], ["tot%d" % t], [])
+
+    def x_rows(t, ph, pl):
+        for f, s in ((4, L("LH", O_N)), (5, L("LL", O_N)), (6, ph), (7, pl)):
+            row("sp", "xr%d" % t, "X", f, s)
+
+    def add_own(t, U):
+        op("pool", lambda: g.dma_start(T[U][:, NW:2 * NW], T[U][:, 0:NW], accum_op=ADD, max_dma_last_dim=4096),
+           [(U, 0, 2 * NW)], [(U, NW, 2 * NW)], grp="vv%d" % t)
+
+    def before_verdict0():
+        for k in range(ZM, len(ZS)):
+            make_z(k)
+        gather("act", "X", ("W", 0, NW), "par16", 0, NW)
+        ts("t1", P("p2"), 0.0, EQ)
+        tt("t2", "t1", "n2560", MUL)
+        tt("t3", P("p2"), "t2", ADD)
+        cp("sc16", "t3")
+        cp("side16", P("p2"))
+        ts(("thb", 0, 1), ("thI", 0, 1), -1.0, MUL, 0.5, ADD)
+        extI("p1", "W", "bit")
+        extI("p0", "W", "i2b", 0, NW, True, False)
+        extI("p3", "W", "bm", 0, NW, True, False)
+        extI("p7", "X", "itm")
+        x_rows(0, L("LH", O_PAR), L("LL", O_PAR))
+        for h in range(2):
+            l = ("sc16", h * 80, (h + 1) * 80)
+            op("dve", lambda l=l, h=h: g.vector.tensor_copy(T.SW[:].indirect(ap(l)), T.W[:, h * H:(h + 1) * H]),
+               [l, ("W", h * H, (h + 1) * H)], ["SW"])
+        gather("act", "SG", ("W", 0, NW), "side16", 0, H)
+        act("sideI", P("p2"))
+        act("bitI", P("p1"))
+        for tt_ in range(2):
+            act(("KW%d" % tt_, NI, NI + 1), ("dcol", 0, 1), AF.Copy)
+
+    def after_verdict0():
+        gather("act", "SG", ("W", 0, NW), "side16", H, NW)
+        cp("ip16", P("p7"))
+        for h in range(2):
+            extI("p0", "SG", "sg0", h * H, (h + 1) * H, False, h == 1)
+            extB("p1", "SG", "side", 8 * h, 8 * h + 8, h == 0, h == 1)
+        extI("p3", "SW", "a0", 0, NW, False, True)
+        extI("p7", "SW", "n")
+        extB("p6", "SW", "n")
+        act("nbB", L("LF", O_BIT), AF.Identity, 1.0, -1.0)
+        act("kaT", P("p0"), AF.Identity, -1024.0)
+        gather("act", "Ua", ("Ua", 0, NW), "par16", 0, NW, shift=NW)
+        add_own(0, "Ua")
+        tt("sA1", "bitI", "sideI", MUL)
+        tt("sA0", "sideI", "sA1", SUB)
+        tt("t1", P("p1"), "nbB", MUL)
+        tt("t3", "t1", L("LF", O_SIDE), SUB)
+        digits("SH", "SL", "t3")
+        tt("t2", P("p3"), "kaT", MIN)
+        ts("ka16", "t2", 3072.0, ADD, 1024.0, MIN)
+        tt("bpI", P("p7"), "bitI", MUL)
+        cp("predI", P("p7"))
+        tt("t3", "bpI", "sA0", ADD)
+        cp("pt16", "t3")
+        tt("eB", P("p6"), L("LF", O_N), SUB)
+        tt("D0", "eB", L("LF", O_BIT), MUL)
+        digits("DH", "DL", "D0")
+
+    def before_verdict1():
+        row("sp", "pr1", "W", R_PAR, "pH")
+        row("sp", "pr1", "W", R_PAR + 1, "pL")
+        extI("p1", "C", "n", 0, NW, True, False)
+        mm(P("p1"), "IDf", "P8I", False, True)
+        cp("par16", P("p1"))
+        gather("act", "C", ("W", 0, NW), "pred16", 0, NW)
+        extI("p3", "W", "bp", 0, NW, True, False)
+        extI("p3", "SW", "a1", 0, NW, False, True)
+        gather("dve", "X", ("W", 0, NW), "par16", 0, NW)
+        gather("dve", "Uc", ("Uc", 0, NW), "par16", 0, NW, shift=NW)
+
+    def after_verdict1():
+        add_own(1, "Uc")
+        extI("p7", "X", "itm")
+        x_rows(1, "pH", "pL")
+        extI("p2", "C", "side")
+        extI("p0", "W", "i2bn", 0, NW, True, False)
+        extI("p0", "SG", "sg1", 0, NW, False, True)
+        cp("ip16", P("p7"))
+        tt("t1", "predI", "bpI", SUB)
+        tt("t3", "eB", "D0", SUB)
+        tt("t2", "t1", "sA1", ADD)
+        digits("DH", "DL", "t3")
+        cp("pt16", "t2")
+        tt("t2", P("p2"), "nI", NE)
+        ts("t1", "mI", 1024.0, MUL, 3072.0, ADD)
+        ts("t3", "t2", 1024.0, MUL, 1024.0, ADD)
+        tt("kaT", P("p0"), "t1", ADD)
+        tt("t1", P("p3"), "t3", ADD)
+        tt("t2", "t1", "kaT", MIN)
+        ts("ka16", "t2", 1024.0, MIN)
+
+    def splice_merge(t, U, U1, U2):
+        kw = ("KW%d" % t, 0, NI + 1)
+        arr = [("ag%d" % t, sum(len(topo.engines(T.cores[r], core)) for r in range(N) if r != rank))]
+        bank = ["p0", "p1"]
+        half = [(0, H), (H, NW)]
+
+        def cvt(lst, h):
+            cp((lst, 80 * h, 80 * (h + 1)), P(bank[h], 80))
+
+        def copy1(j):
+            a, b = TAIL[j]
+            dma("sp", "ud%d_%d" % (t, j), T.Ud[:, a:b], T[U1][:, a:b], [(U1, a, b)], [("Ud", a, b)])
+        mm(P("p5"), "IDf", "n2560", True, False)
+        mm(P("p2"), "IDb", "zB", True, False)
+        for h in range(2):
+            gather("dve", "A", kw, "ip16", half[h][0], half[h][1], "X", MUL, ext=arr)
+            extI(bank[h], "A", "r", half[h][0], half[h][1], o=0)
+            extI("p5", "A", "kp", half[h][0], half[h][1], False, h == 1)
+        gather("act", "KA", kw, "ka16", 0, NW, ext=arr)
+        cvt("j1", 0)
+        chain = [("B", "A", "j1", "j2"), ("A", "B", "j2", "j4l"), ("B", "A", "j4l", None)]
+        for lv, (o, win, lst, nxt) in enumerate(chain):
+            for h in range(2):
+                a, b = half[h]
+                gather("act", o, win, lst, a, a + SPLIT)
+                gather("dve", o, win, lst, a + SPLIT, b)
+                if h == 0:
+                    cvt(lst, 1)
+                if nxt:
+                    extI(bank[h], o, "r", a, b, o=0)
+                    if lv == 0:
+                        extB("p3", "KA", "drop", 8 * h, 8 * h + 8, h == 0, False)
+                    else:
+                        extI("p2", "KA", "drop", a, b, False, False)
+                else:
+                    extB("p4", o, "j", 8 * h, 8 * h + 8, h == 0, h == 1)
+                    extI("p6", o, "j", a, b)
+            if nxt:
+                cvt(nxt, 0)
+            if lv == 0:
+                cp("pe16", P("p5"))
+        for h in range(2):
+            a, b = half[h]
+            gather("act", "C", "B", "pt16", a, a + PSPLIT)
+            gather("dve", "C", "B", "pt16", a + PSPLIT, b)
+            extB("p3", "C", "j", 8 * h, 8 * h + 8, False, h == 1)
+        extI("p2", "C", "j", 0, NW, False, True)
+        for a, b in TAIL:
+            gather("act", U1, U, "pe16", a, b)
+        copy1(0)
+        cp("P8B", P("p4"))
+        cp("P8I", P("p6"))
+        cp("p816", P("p6"))
+        tt("mB", P("p3"), "P8B", EQ)
+        tt("dH", "mB", "DH", MUL)
+        row("sp", "rp%d" % t, "A", R_N, "dH")
+        tt("dL", "mB", "DL", MUL)
+        row("sp", "rp%d" % t, "A", R_N + 1, "dL")
+        copy1(1)
+        if t == 0:
+            tt("sH", "mB", "SH", MUL)
+            row("sp", "sd1", "W", R_DS, "sH")
+            tt("sL", "mB", "SL", MUL)
+            row("sp", "sd1", "W", R_DS + 1, "sL")
+        copy1(2)
+        copy1(3)
+        tt("mI", P("p2"), "P8I", EQ)
+        tt("t1", "mI", "sA%d" % t, MUL)
+        cp("se16", "t1")
+        mm(P("p3"), "IDf", "P8B", True, False)
+        for j, (a, b) in enumerate(TAIL):
+            gather("act", "C", "A", "p816", a, b)
+            gather("dve", U2, U1, "se16", a, b, "Ud", ADD)
+            extB("p3", "C", "n", a // NC, b // NC, False, b == NW)
+            if t == 1:
+                ts(("Y", a, b), (U2, a, b), 15.0, MIN)
+                dma("sp", "yc%d" % j, T.yc[:, a:b], T.Y[:, a:b], [("Y", a, b)], [])
+        if t == 0:
+            ge4(U2, 800, 1760, True)
+            ge4(U2, 0, 800, False, "act")
+            ge4(U2, 1760, NW, False)
+            digits("pH", "pL", P("p3"))
+        else:
+            act("ypB", P("p3"))
+            dma("act", "yp0", T.yp[:], T.ypB[:], ["ypB"], [])
+
+    prep(0, "Ua")
+    walks(0)
+    before_verdict0()
+    verdict(0)
+    after_verdict0()
+    splice_merge(0, "Ua", "Ub", "Uc")
+    prep(1, "Uc")
+    walks(1)
+    before_verdict1()
+    verdict(1)
+    after_verdict1()
+    splice_merge(1, "Uc", "Ub", "Ua")
+
+    total = {}
+    for o in ops:
+        if o["grp"]:
+            total["d_" + o["grp"]] = total.get("d_" + o["grp"], 0) + 16
+    count = {}
+    for o in ops:
+        if o["grp"]:
+            o["done"] = ("d_" + o["grp"], total["d_" + o["grp"]])
+        elif o["inc"]:
+            s = "e_" + o["e"]
+            count[s] = count.get(s, 0) + 1
+            o["done"] = (s, count[s])
+        else:
+            o["done"] = None
+    total.update(count)
+
+    def meet(a, b):
+        return a[1] < b[2] and b[1] < a[2] and (a[3] is None or b[3] is None or a[3] == b[3])
+
+    seen = {}
+    waited = {}
+    for o in ops:
+        need = {}
+        for s, v in o["ext"]:
+            need[s] = v
+        acc_ = [(x, False) for x in o["r"]] + [(x, True) for x in o["w"]]
+        for x, wr in acc_:
+            psum = SCRATCH[x[0]][0] == "psum"
+            for y, ywr, q in seen.get(x[0], []):
+                if q["done"] is None or (q["grp"] and q["grp"] == o["grp"]):
+                    continue
+                same = q["e"] == o["e"] and not q["grp"] and not o["grp"]
+                if same and o["e"] == "pe":
+                    continue
+                if (psum and not same) or ((wr or ywr) and meet(x, y)):
+                    s, v = q["done"]
+                    need[s] = max(need.get(s, 0), v)
+        for x, wr in acc_:
+            seen.setdefault(x[0], []).append((x, wr, o))
+        for s in sorted(need):
+            if waited.get((o["e"], s), 0) < need[s]:
+                Q[o["e"]].wait_ge(T.sem[s], need[s])
+                waited[(o["e"], s)] = need[s]
+        ins = o["fn"]()
+        if o["done"]:
+            ins.then_inc(T.sem[o["done"][0]], 16 if o["grp"] else 1)
+    total["sent"] = sent[0]
+    for s in sorted(total):
+        g.wait_ge(T.sem[s], total[s])

@@ -10,46 +10,45 @@ def pair(r, w=1.0):
     return {r: w, r + 1: w}
 
 
-def join(*ds):
-    o = {}
-    for d in ds:
-        o.update(d)
-    return o
+def sigma(w):
+    return {0: w / 16, 1: 160 * w, 2: w / 16, 3: 160 * w}
 
 
-SIDE = join(pair(R_SIDE), pair(R_DS))
 ZS = [
-    ("all", None),
-    ("head", pair(R_DS)),
-    ("side", SIDE),
-    ("x", join(SIDE, {R_UP: 4096.0})),
-    ("lin", join(pair(R_PU), SIDE, {R_UP: 2560.0})),
-    ("par", pair(R_PAR)),
-    ("lin0", join(pair(R_PU), SIDE)),
-    ("bit", {R_BIT: 1.0}),
-    ("i2b", join(pair(R_ITM), {R_BIT: 2048.0})),
-    ("bm", {R_BIT: -2048.0}),
-    ("itm", pair(R_ITM)),
-    ("sg0", {R_BIT: -1024.0, R_NZ: -1024.0}),
-    ("a0", join(pair(R_ITM), {R_BIT: 1024.0, R_ONE: -1024.0})),
-    ("n", pair(R_N)),
-    ("j", join(pair(0), pair(2))),
-    ("r", join(pair(4), pair(6))),
-    ("kp", {R_ONE: -2560.0}),
-    ("drop", {2: 4096.0}),
-    ("i2bn", join(pair(R_ITM), {R_BIT: -2048.0})),
-    ("sg1", {R_BIT: 1024.0, R_NZ: -1024.0}),
-    ("a1", join(pair(R_ITM), {R_BIT: -1024.0})),
-    ("bp", {R_BIT: 2048.0}),
+    ("all", None, None),
+    ("n", None, pair(R_N)),
+    ("side", None, {R_SIDE: 1.0, R_SIDE + 1: 1.0, R_DS: 1.0, R_DS + 1: 1.0}),
+    ("x", "side", {R_UP: 4096.0}),
+    ("lin0", "side", pair(R_PU)),
+    ("lin", "lin0", {R_UP: 2560.0}),
+    ("par", None, pair(R_PAR)),
+    ("sb0", "side", {R_BIT: -4096.0}),
+    ("itm", None, pair(R_ITM)),
+    ("i2b", "itm", {R_BIT: 2048.0}),
+    ("sg0", None, {R_BIT: -1024.0, R_NZ: -1024.0}),
+    ("a0", "itm", {R_BIT: 1024.0, R_ONE: -1024.0}),
+    ("pd", None, pair(6)),
+    ("r", "pd", pair(4)),
+    ("kp", None, {R_ONE: -2560.0}),
+    ("drop", None, {2: 2.0 ** 24}),
+    ("jzm", None, sigma(-4096.0)),
+    ("jzp", None, sigma(4096.0)),
+    ("js", None, sigma(1.0)),
+    ("jn", "n", pair(2)),
+    ("sb1", "side", {R_BIT: 4096.0}),
+    ("i2bn", "itm", {R_BIT: -2048.0}),
+    ("sg1", None, {R_BIT: 1024.0, R_NZ: -1024.0}),
+    ("a1", "itm", {R_BIT: -1024.0}),
 ]
 ZI = {z[0]: k for k, z in enumerate(ZS)}
 ZE = 7
-ZM = 11
 ZW = 144
+UA = 1600
 
 SCRATCH = {}
-for _n in ("Ub", "A", "B", "C", "KA", "GE", "Y", "UM", "SG", "X", "Ud"):
+for _n in ("A", "B", "C", "KA", "GE", "Y", "UM", "SG", "X", "Ud"):
     SCRATCH[_n] = ("sbuf", [128, NW], "bfloat16")
+SCRATCH["Ub"] = ("sbuf", [128, NW + 16], "bfloat16")
 for _n in ("W", "SW", "Ua", "Uc"):
     SCRATCH[_n] = ("sbuf", [128, 2 * NW], "bfloat16")
 for _n in ("F0", "F1", "G0", "G1", "G2", "S", "ACC0", "ACC1", "LAND0", "LAND1"):
@@ -57,21 +56,24 @@ for _n in ("F0", "F1", "G0", "G1", "G2", "S", "ACC0", "ACC1", "LAND0", "LAND1"):
 for _n in ("KW0", "KW1"):
     SCRATCH[_n] = ("sbuf", [128, NI + 16], "bfloat16")
 SCRATCH["ZZ"] = ("sbuf", [128, len(ZS) * ZW], "bfloat16")
-for _n in ("IDb", "BO", "s1", "s2", "c15"):
+SCRATCH["BZ"] = ("sbuf", [128, 16 * 128], "bfloat16")
+for _n in ("IDb", "NId", "M2", "BO", "s1", "s2", "c15"):
     SCRATCH[_n] = ("sbuf", [128, 128], "bfloat16")
 for _n in ("IDf", "tot0", "tot1"):
     SCRATCH[_n] = ("sbuf", [128, 128], "float32")
-O_SIDE, O_HEAD, O_PAR, O_ITM, O_N, O_BIT, O_END = 0, 160, 224, 384, 544, 704, 864
-SCRATCH["LI"] = ("sbuf", [128, O_END], "int32")
-SCRATCH["LF"] = ("sbuf", [128, O_END], "float32")
-SCRATCH["LH"] = ("sbuf", [128, O_END], "bfloat16")
-SCRATCH["LL"] = ("sbuf", [128, O_END], "bfloat16")
-for _n in ("nI", "n2560", "sideI", "bitI", "predI", "sA0", "sA1", "t1", "t2", "t3", "P8I", "P8B", "mI",
-           "D0", "eB", "nbB", "ypB", "kaT", "bpI"):
+O_HEAD, O_PAR, O_SIDE, O_ITM, O_BIT, O_END = 0, 64, 224, 384, 544, 704
+for _n in ("LI", "HI"):
+    SCRATCH[_n] = ("sbuf", [128, O_END], "int32")
+for _n in ("LH", "LL"):
+    SCRATCH[_n] = ("sbuf", [128, O_END], "bfloat16")
+for _n in ("nI", "n2560", "npre", "predI", "sA0", "sA1", "t1", "t2", "t3", "ypB", "kaT", "bpI", "pB"):
     SCRATCH[_n] = ("sbuf", [128, NC], "float32")
-for _n in ("upB", "puH", "puL", "dH", "dL", "sH", "sL", "pH", "pL", "DH", "DL", "mB", "SH", "SL", "zB"):
+for _n in ("pJ", "pK"):
+    SCRATCH[_n] = ("sbuf", [128, NC], "int32")
+for _n in ("upB", "puH", "puL", "dH", "dL", "sH", "sL", "pH", "pL", "qH", "qL", "DH", "DL", "mB", "mI", "SH", "SL", "bitI",
+           "nbI", "z0", "nBH", "nBL", "nIH", "nIL", "cB", "nzB", "oneB"):
     SCRATCH[_n] = ("sbuf", [128, NC], "bfloat16")
-for _n in ("par16", "side16", "ip16", "sc16", "ka16", "pt16", "pred16", "j1", "j2", "j4l", "pe16", "p816", "se16"):
+for _n in ("par16", "side16", "ip16", "sc16", "ka16", "pt16", "j1", "j2", "j4l", "pe16", "p816", "se16"):
     SCRATCH[_n] = ("sbuf", [128, NC], "uint16")
 for _n in ("hd16", "ix1", "ix2", "w1", "w2", "w3"):
     SCRATCH[_n] = ("sbuf", [128, 64], "uint16")
@@ -81,25 +83,28 @@ for _n in ("thI", "pI", "fI", "fH"):
     SCRATCH[_n] = ("sbuf", [128, 4], "int32")
 for _n in ("thb", "fF", "f160", "dcol", "scol"):
     SCRATCH[_n] = ("sbuf", [128, 4], "float32")
+SCRATCH["OH"] = ("sbuf", [128, 16], "float32")
 SCRATCH["z8"] = ("sbuf", [128, 8], "bfloat16")
 for _k in range(8):
     SCRATCH["p%d" % _k] = ("psum", [128, 512], "float32")
 
 ENG = ["pe", "dve", "act", "pool"]
-DMAG = ["ld", "ldu0", "ldu1", "ldth", "hd0", "wa0", "fw0", "fx0", "fw1", "fx1", "rp0", "rp1", "sd1", "pr1", "vv0", "xr0",
-        "xr1", "ya0", "ya1", "yc0", "yc1", "yc2", "yc3", "yp0", "vv1"] + \
-    ["ud%d_%d" % (_t, _j) for _t in range(2) for _j in range(4)]
+DMAG = ["ldh", "ldp", "ldi", "ldu0", "ldu1", "ldu2", "ldu3", "ldth", "hd0", "late", "swz", "fw0", "fx0", "fw1", "fx1", "rp0", "rp1",
+        "sd1", "pr1", "vv0", "vv1", "xr0", "xr1", "ya0", "ya1", "yc0", "yc1", "yc2", "yc3", "yp0", "uu0", "uu1"] + \
+    ["ud%d_%d" % (_t, _j) for _t in range(2) for _j in (0, 2, 3)]
 SEMAPHORES = ["e_" + _e for _e in ENG] + ["d_" + _d for _d in DMAG] + ["sent"] + \
     ["rs%d_%d" % (_t, _m) for _t in range(2) for _m in range(4)] + ["ag0", "ag1"]
 
 ADD, SUB, MUL, MAX, MIN = AluOpType.add, AluOpType.subtract, AluOpType.mult, AluOpType.max, AluOpType.min
-GE_, EQ, NE = AluOpType.is_ge, AluOpType.is_equal, AluOpType.not_equal
+GE_, LT, EQ, NE = AluOpType.is_ge, AluOpType.is_lt, AluOpType.is_equal, AluOpType.not_equal
 AND = AluOpType.bitwise_and
 AF = ActivationFunctionType
 SPLIT = 672
 PSPLIT = 640
-CUT = (768, 640, 544)
+CUT = ((768, 768, 768), (704, 704, 640))
 TAIL = [(640 * _j, 640 * (_j + 1)) for _j in range(4)]
+HALF = [(0, H), (H, NW)]
+PIECE = [(UA, 2080), (0, 800), (2080, NW), (800, UA)]
 
 
 def rank_program(g, core, T, topo):
@@ -126,13 +131,19 @@ def rank_program(g, core, T, topo):
             return T[x[0]][:]
         return T[x[0]][:, x[1]:x[2]]
 
+    def col(s):
+        if isinstance(s, str):
+            return T[s][:, 0:1], [s]
+        if isinstance(s, tuple):
+            return ap(s), [s]
+        return s, []
+
     def ts(o, i, s1, op0, s2=None, op1=None):
-        a1 = T[s1][:, 0:1] if isinstance(s1, str) else s1
-        rd = [i] + ([s1] if isinstance(s1, str) else [])
+        a1, rd = col(s1)
         if op1 is None:
-            op("dve", lambda: g.vector.tensor_scalar(ap(o), ap(i), a1, None, op0), rd, [o])
+            op("dve", lambda: g.vector.tensor_scalar(ap(o), ap(i), a1, None, op0), [i] + rd, [o])
         else:
-            op("dve", lambda: g.vector.tensor_scalar(ap(o), ap(i), a1, s2, op0, op1), rd, [o])
+            op("dve", lambda: g.vector.tensor_scalar(ap(o), ap(i), a1, s2, op0, op1), [i] + rd, [o])
 
     def tt(o, a, b, alu):
         op("dve", lambda: g.vector.tensor_tensor(ap(o), ap(a), ap(b), alu), [a, b], [o])
@@ -144,19 +155,18 @@ def rank_program(g, core, T, topo):
         op("dve", lambda: g.vector.memset(ap(o), v), [], [o])
 
     def act(o, i, func=AF.Identity, bias=0.0, scale=1.0):
-        b = T[bias][:, 0:1] if isinstance(bias, str) else bias
-        s = T[scale][:, 0:1] if isinstance(scale, str) else scale
-        rd = [i] + [x for x in (bias, scale) if isinstance(x, str)]
-        op("act", lambda: g.scalar.activation(ap(o), ap(i), func, bias=b, scale=s), rd, [o])
+        b, rb = col(bias)
+        s, rs = col(scale)
+        op("act", lambda: g.scalar.activation(ap(o), ap(i), func, bias=b, scale=s), [i] + rb + rs, [o])
 
-    def gather(eng, o, win, lst, a, b, in1=None, alu=None, ext=(), shift=0):
+    def gather(eng, o, win, lst, a, b, in1=None, alu=None, ext=(), shift=0, shift1=0):
         l = (lst, a // 16, b // 16)
         out = (o, shift + a, shift + b)
-        rd = [win, l] + ([(in1, a, b)] if in1 else [])
+        rd = [win, l] + ([(in1, shift1 + a, shift1 + b)] if in1 else [])
         if eng == "act":
             fn = lambda: g.scalar.activation(ap(out), ap(win).indirect(ap(l)), AF.Copy)
         elif in1:
-            fn = lambda: g.vector.tensor_tensor(ap(out), ap(win).indirect(ap(l)), T[in1][:, a:b], alu)
+            fn = lambda: g.vector.tensor_tensor(ap(out), ap(win).indirect(ap(l)), ap(rd[2]), alu)
         else:
             fn = lambda: g.vector.tensor_copy(ap(out), ap(win).indirect(ap(l)))
         op(eng, fn, rd, [out], ext=ext)
@@ -186,24 +196,36 @@ def rank_program(g, core, T, topo):
             return ins
         op("pe", fn, [(src, NC * i0, NC * i1), zreg(z)], [bank])
 
+    def spread(bank, src, i0, i1, lhs=None, win=None):
+        if win:
+            mm(P(bank, NC * (i1 - i0)), lhs, (win, NC * i0, NC * i1), True, False)
+
+        def fn():
+            for i in range(i0, i1):
+                ins = g.tensor.matmul(T[bank][:, NC * (i - i0):NC * (i - i0 + 1)], T.BZ[:, 128 * i:128 * (i + 1)], T[src][:],
+                                      not win, not win or i == i1 - 1)
+            return ins
+        op("pe", fn, [src, ("BZ", 128 * i0, 128 * i1)], [bank])
+
     def mm(o, lhs, rhs, start, stop, ext=()):
         op("pe", lambda: g.tensor.matmul(ap(o), T[lhs][:], ap(rhs), start, stop), [lhs, rhs], [o], ext=ext)
 
-    def dma(q, grp, out, in_, r, w):
-        op(q, lambda: Q[q].dma_start(out, in_), r, w, grp=grp)
+    def dma(q, grp, out, in_, r, w, ext=()):
+        op(q, lambda: Q[q].dma_start(out, in_), r, w, grp=grp, ext=ext)
 
-    def row(q, grp, win, f, src, c0=0, n=NW):
-        dma(q, grp, T[win][f::16, c0:c0 + n], ap(src), [src], [(win, c0, c0 + n, f)])
-
-    def digits(hi, lo, v):
-        cp(hi, v)
-        tt(lo, v, hi, SUB)
+    def row(q, grp, win, f, src, c0=0, n=NW, ext=()):
+        dma(q, grp, T[win][f::16, c0:c0 + n], ap(src), [src], [(win, c0, c0 + n, f)], ext)
 
     def P(bank, n=NC, o=0):
         return (bank, o, o + n)
 
     def L(buf, o, n=NC):
         return (buf, o, o + n)
+
+    def digits(o, n):
+        ts(L("HI", o, n), L("LI", o, n), 0xFF0, AND)
+        cp(L("LH", o, n), L("HI", o, n))
+        tt(L("LL", o, n), L("LI", o, n), L("HI", o, n), SUB)
 
     def dst(r):
         rid, pid = topo.addr(T.cores[r], core)
@@ -217,7 +239,7 @@ def rank_program(g, core, T, topo):
     def bits(e):
         return sum(1 << x for x in e)
 
-    def iota(o, pat, cm, small):
+    def iota(o, pat, cm=0, small=True):
         if small:
             op("pool", lambda: g.iota(ap(o), pat, 0, cm, allow_small_or_imprecise_dtypes=True), [], [o])
         else:
@@ -226,60 +248,68 @@ def rank_program(g, core, T, topo):
     def asel(o, oap, i, iap, pat, cmp, fill, base, cm):
         op("pool", lambda: g.affine_select(oap, iap, pat, cmp, fill, base, cm), [i], [o])
 
-    def make_z(k):
-        name, wts = ZS[k]
-        v = T.ZZ[:, k * ZW + 16:(k + 1) * ZW:16]
-        if wts is None:
-            asel("z8", T.z8[:], "IDb", T.IDb[:, 0:8], [[-16, 8]], GE_, 0.0, 0, 1)
-            asel(zreg(name), v, "z8", T.z8[:], [[16, 8]], GE_, 0.0, 15, -1)
-        else:
-            for f in sorted(wts):
-                asel(zreg(name), v, zreg(name), v, [[-16, 8]], NE, wts[f], -f, 1)
+    def make_z(*names):
+        view = lambda z: T.ZZ[:, ZI[z] * ZW + 16:(ZI[z] + 1) * ZW:16]
+        for name in names:
+            _, base, wts = ZS[ZI[name]]
+            if wts is None:
+                asel("z8", T.z8[:], "IDb", T.IDb[:, 0:8], [[-16, 8]], GE_, 0.0, 0, 1)
+                asel(zreg(name), view(name), "z8", T.z8[:], [[16, 8]], GE_, 0.0, 15, -1)
+            else:
+                src = base or name
+                for f in sorted(wts):
+                    asel(zreg(name), view(name), zreg(src), view(src), [[-16, 8]], NE, wts[f], -f, 1)
+                    src = name
 
     def zero(o, i):
         act(o, i, AF.Identity, 0.0, 0.0)
 
-    for name, o, n in (("side", O_SIDE, NC), ("heads", O_HEAD, 64), ("par", O_PAR, NC), ("itm", O_ITM, NC), ("bit", O_BIT, NC)):
-        dma("sp", "ld", T.LI[:, o:o + n], T[name][:], [], [L("LI", o, n)])
-    dma("act", "ldu0", T.Ua[:, 0:H], T.cnt[:, 0:H], [], [("Ua", 0, H)])
-    dma("act", "ldu1", T.Ua[:, H:NW], T.cnt[:, H:NW], [], [("Ua", H, NW)])
+    def load(q, grp, name, o, n):
+        dma(q, grp, T.LI[:, o:o + n], T[name][:], [], [L("LI", o, n)])
+
+    load("sp", "ldh", "heads", O_HEAD, 64)
+    load("act", "ldp", "par", O_PAR, NC)
+    load("sp", "ldp", "side", O_SIDE, NC)
+    for j, (a, b) in enumerate(TAIL):
+        dma("act" if j % 2 == 0 else "sp", "ldu%d" % j, T.Ua[:, a:b], T.cnt[:, a:b], [], [("Ua", a, b)])
+    load("sp", "ldi", "itm", O_ITM, NC)
+    load("sp", "ldi", "bit", O_BIT, NC)
     iota(("pI", 0, 1), [[0, 1]], 1, False)
-    iota(L("LF", O_N), [[1, NC]], 0, True)
-    iota("nI", [[16, NC]], 0, True)
-    ms(("W", 0, 640), 1.0)
-    ms(("ZZ", 0, ZE * ZW), 0.0)
-    ms("IDb", 1.0)
+    iota("OH", [[1, 16]])
     ms("c15", 15.0)
-    act(("W", 640, 1280), ("W", 0, 640), AF.Copy)
-    act(("W", 1280, NW), ("W", 0, 1280), AF.Copy)
-    make_z(0)
-    asel("BO", T.BO[:], "c15", T.c15[:], [[-16, 8], [0, 16]], GE_, 0.0, 0, 1)
-    asel("BO", T.BO[:], "BO", T.BO[:], [[16, 8], [0, 16]], GE_, 0.0, 15, -1)
-    make_z(1)
-    asel("IDb", T.IDb[:], "IDb", T.IDb[:], [[-1, 128]], EQ, 0.0, 0, 1)
-    for k in range(2, ZE):
-        make_z(k)
-    iota(("ZZ", ZE * ZW, len(ZS) * ZW), [[0, (len(ZS) - ZE) * ZW]], 0, True)
-    op("pool", lambda: g.dma_start(T.thI[:, 0:1], T.th[:], allow_slow_non_contiguous=True), [], [("thI", 0, 1)], grp="ldth")
-    for k in range(ZE, ZM):
-        make_z(k)
+    ms("IDb", 1.0)
+    ms(("ZZ", 0, ZE * ZW), 0.0)
+    ms(("W", NW, NW + H), 0.0)
     ts(("fI", 0, 1), ("pI", 0, 1), 15, AND)
     cp(("fF", 0, 1), ("fI", 0, 1))
-    ts(("fH", 0, 1), ("pI", 0, 1), 10, AND)
-    ts(("f160", 0, 1), ("fF", 0, 1), 160.0, MUL)
-    ts(("dcol", 0, 1), ("fH", 0, 1), 2.0, EQ)
-    ts(L("LF", O_N), L("LF", O_N), "f160", ADD)
-    ts(("scol", 0, 1), ("dcol", 0, 1), -2.0, MUL, 1.0, ADD)
-    ms("zB", 0.0)
-    ts("nI", "nI", "fF", ADD)
-    ts("n2560", "nI", float(NW), ADD)
-    cp(("LF", 0, O_N), ("LI", 0, O_N))
-    cp(L("LF", O_BIT), L("LI", O_BIT))
-    ts(("W", 0, 1), ("fF", 0, 1), float(R_NZ), NE)
-    act("LH", "LF", AF.Copy)
-    row("sp", "wa0", "W", R_DS, "zB")
-    row("sp", "wa0", "W", R_DS + 1, "zB")
-    zero(("SW", 0, H), ("Ua", 0, H))
+    ts("OH", "OH", "fF", EQ)
+    ms(("W", 0, NW), 0.0)
+    asel("BO", T.BO[:], "c15", T.c15[:], [[-16, 8], [0, 16]], GE_, 0.0, 0, 1)
+    asel("BO", T.BO[:], "BO", T.BO[:], [[16, 8], [0, 16]], GE_, 0.0, 15, -1)
+    make_z("all", "par")
+    act(("W", NW + H, 2 * NW), ("W", NW, NW + H), AF.Copy)
+    for i in range(10):
+        act(("BZ", 128 * i, 128 * (i + 1)), "BO", AF.Identity, 0.0, ("OH", i, i + 1))
+    asel("IDb", T.IDb[:], "IDb", T.IDb[:], [[-1, 128]], EQ, 0.0, 0, 1)
+    for i in range(10, 16):
+        z = ("BZ", 128 * i, 128 * (i + 1))
+        asel(z, ap(z), "c15", T.c15[:], [[-16, 8], [0, 16]], EQ, 0.0, -i, 1)
+    make_z("side", "x", "lin0", "lin")
+    iota("nI", [[16, NC]])
+    iota("cB", [[1, NC]])
+    iota("nBL", [[0, 10], [1, 16]])
+    iota("nBH", [[16, 10], [0, 16]])
+    iota("nIH", [[16, NC]])
+    op("pool", lambda: g.dma_start(T.thI[:, 0:1], T.th[:], allow_slow_non_contiguous=True), [], [("thI", 0, 1)], grp="ldth")
+    iota(("ZZ", ZE * ZW, len(ZS) * ZW), [[0, (len(ZS) - ZE) * ZW]])
+    make_z("n", "sb0", "itm", "i2b", "sg0", "a0")
+    digits(O_HEAD, 64)
+    row("sp", "hd0", "W", R_PAR, L("LH", O_HEAD, 64), NW, NI)
+    row("sp", "hd0", "W", R_PAR + 1, L("LL", O_HEAD, 64), NW, NI)
+    digits(O_PAR, 2 * NC)
+    for f, o in ((R_SIDE, O_SIDE), (R_PAR, O_PAR)):
+        row("sp", "fw0", "W", f, L("LH", o))
+        row("sp", "fw0", "W", f + 1, L("LL", o))
 
     def ge4(U, a, b, first, eng="dve"):
         if eng == "dve":
@@ -290,47 +320,38 @@ def rank_program(g, core, T, topo):
 
     def prep(t, U):
         if t == 0:
-            ge4(U, 0, H, True)
-            ge4(U, H, NW, False)
-            tt(("LL", 0, O_BIT), ("LF", 0, O_BIT), ("LH", 0, O_BIT), SUB)
-            row("sp", "wa0", "W", R_BIT, L("LH", O_BIT))
-            for f, o in ((R_SIDE, O_SIDE), (R_PAR, O_PAR), (R_ITM, O_ITM), (R_N, O_N)):
-                row("sp", "wa0", "W", f, L("LH", o))
-            row("sp", "hd0", "SW", R_DS, L("LH", O_HEAD, 64), 0, NI)
-            row("sp", "hd0", "SW", R_DS + 1, L("LL", O_HEAD, 64), 0, NI)
-            for f, o in ((R_SIDE, O_SIDE), (R_PAR, O_PAR), (R_ITM, O_ITM), (R_N, O_N)):
-                row("sp", "wa0", "W", f + 1, L("LL", o))
-            zero(("W", NW, NW + H), ("Ua", 0, H))
+            for j, (a, b) in enumerate(TAIL):
+                ge4(U, a, b, a == 0, "act" if j == 1 else "dve")
+            extI("p1", "W", "par", NW, NW + NI, o=0)
             ph, pl = L("LH", O_PAR), L("LL", O_PAR)
         else:
             ph, pl = "pH", "pL"
         ts("upB", P("p0"), 0.5, GE_)
-        row("act", "fw%d" % t, "W", R_UP, "upB")
+        row("sp", "fw%d" % t, "W", R_UP, "upB")
         tt("puH", ph, "upB", MUL)
         row("sp", "fw%d" % t, "W", R_PU, "puH")
         tt("puL", pl, "upB", MUL)
         row("sp", "fw%d" % t, "W", R_PU + 1, "puL")
-        if t == 0:
-            zero(("W", NW + H, 2 * NW), ("Ua", H, NW))
-            zero(("SW", H, NW), ("Ua", H, NW))
         for f, s in ((R_UP, "upB"), (R_PU, "puH"), (R_PU + 1, "puL")):
             row("sp", "fx%d" % t, "W", f, s, NW)
-        for c in range(5):
-            b = "p%d" % (4 + c % 2)
-            mm(b, "BO", ("GE", 512 * c, 512 * (c + 1)), True, True)
-            tt(("Y", 512 * c, 512 * (c + 1)), b, (U, 512 * c, 512 * (c + 1)), MIN)
-            if t == 0 and c == 3:
-                extI("p1", "SW", "head", 0, NI)
-                cp("hd16", P("p1", 64))
         if t == 0:
-            cp("IDf", "IDb")
-            extI("p2", "W", "side")
+            cp("hd16", P("p1", 64))
+            act("IDf", "IDb")
+            act("M2", "IDb", AF.Identity, 0.0, -2048.0)
+            act("NId", "IDb", AF.Identity, 0.0, -1.0)
+            dma("sp", "swz", T.SW[:, 0:NW], T.W[:, NW:2 * NW], [("W", NW, 2 * NW)], [("SW", 0, NW)])
+        for (i0, i1), (k0, k1), b, c in (((0, 3), (9, 12), "p5", "p6"), ((3, 6), (12, 14), "p4", "p7"),
+                                         ((6, 9), (14, 16), "p5", "p6")):
+            spread(b, "upB", i0, i1)
+            tt(("UM", NC * i0, NC * i1), P(b, NC * (i1 - i0)), (U, NC * i0, NC * i1), MIN)
+            spread(c, "upB", k0, k1, "NId" if t else "IDb", "Y" if t else U)
+            act(("UM", NC * k0, NC * k1), P(c, NC * (k1 - k0)), AF.Relu, 0.0 if t else -15.0)
 
-    def walks(t):
+    def walks(t, pe_fill, dve_fill, act_fill, after_f, in_sums):
         acc = "ACC%d" % t
-        gather("act", "F0", ("W", 0, NW), "hd16", 0, NI)
-        for h in range(2):
-            ts(("UM", h * H, (h + 1) * H), ("Y", h * H, (h + 1) * H), 0.0, MAX, 15.0, MIN)
+        gather("act", "F0", ("W", 0, NW), "hd16", 0, 512)
+        gather("dve", "F0", ("W", 0, NW), "hd16", 512, NI)
+        pe_fill[0]()
         lists = ["hd16", "w1", "w2", "w3"]
         for s in range(3):
             k, F = "k%d" % s, "F%d" % (s % 2)
@@ -338,10 +359,9 @@ def rank_program(g, core, T, topo):
                 if s > 0:
                     mm(P(bank, 64), "IDf", "k%d" % (s - 1), True, False)
                 extI(bank, F, z, 0, NI, s == 0, True)
-            if s == 0 and t == 0:
-                extI("p3", "W", "par")
-            gather("act", "G%d" % s, "UM", lists[s], 0, CUT[s])
-            gather("dve", "G%d" % s, "UM", lists[s], CUT[s], NI)
+            gather("act", "G%d" % s, "UM", lists[s], 0, CUT[t][s])
+            gather("dve", "G%d" % s, "UM", lists[s], CUT[t][s], NI)
+            dve_fill[s]()
             ts(k, P("p0", 64), -4096.0, ADD, 0.0, MAX)
             if s < 2:
                 ts("wu", P("p0", 64), 4096.0, GE_, float(NW), MUL)
@@ -349,16 +369,16 @@ def rank_program(g, core, T, topo):
             cp("ix%d" % (s + 1) if s < 2 else "w3", "wa")
             for h in range(2):
                 mm("p%d" % (6 + h), "IDb", ("G%d" % s, 512 * h, 512 * (h + 1)), s == 0, s == 2)
+            pe_fill[s + 1]()
+            act_fill[s]()
             if s < 2:
                 F = "F%d" % ((s + 1) % 2)
                 tt("wb", "wa", "wu", SUB)
                 gather("act", F, "W", "ix%d" % (s + 1), 0, 512)
                 gather("dve", F, "W", "ix%d" % (s + 1), 512, NI)
                 cp(lists[s + 1], "wb")
-        if t == 0:
-            cp("par16", P("p3"))
-        else:
-            cp("pred16", "predI")
+                if s == 1:
+                    after_f()
         order = [(rank // 2 + m) % 4 for m in (1, 2, 3, 0)]
         for c in order:
             act(("S", 256 * c, 256 * (c + 1)), ("p%d" % (6 + c // 2), 256 * (c % 2), 256 * (c % 2 + 1)), AF.Copy)
@@ -373,17 +393,26 @@ def rank_program(g, core, T, topo):
                 return g.remote_dma_fused(tr, local_sem=T.sem.sent)
             sent[0] += sum(len(engs(r, j, len(to))) for j, r in enumerate(to))
             op("pool", send, [(acc, 256 * c, 256 * (c + 1))], [], inc=False)
+            if m == 1:
+                in_sums()
+
+    def senders(m):
+        c = (rank // 2 - (m + 1)) % 4
+        return [r for r in (2 * c, 2 * c + 1) if r != rank]
+
+    def sums_in(t, m):
+        return ("rs%d_%d" % (t, m), sum(len(topo.engines(T.cores[r], core)) // len(senders(m)) for r in senders(m)))
+
+    def verdicts_in(t):
+        return ("ag%d" % t, sum(len(topo.engines(T.cores[r], core)) for r in range(N) if r != rank))
 
     def verdict(t):
         acc, land, kw = "ACC%d" % t, "LAND%d" % t, "KW%d" % t
         own = (128 * rank, 128 * (rank + 1))
         mm(P("p4", 128), "IDb", (acc,) + own, True, False)
         for m in range(4):
-            c = (rank // 2 - (m + 1)) % 4
-            frm = [r for r in (2 * c, 2 * c + 1) if r != rank]
-            cnt = sum(len(topo.engines(T.cores[r], core)) // len(frm) for r in frm)
-            for r in frm:
-                mm(P("p4", 128), "IDb", (land, 128 * r, 128 * (r + 1)), False, m == 3, ext=[("rs%d_%d" % (t, m), cnt)])
+            for r in senders(m):
+                mm(P("p4", 128), "IDb", (land, 128 * r, 128 * (r + 1)), False, m == 3, ext=[sums_in(t, m)])
         act("s1", P("p4", 128), AF.Sign, "thb")
         mm(P("p5", 128), "BO", "s1", True, True)
         act("s2", P("p5", 128), AF.Sign, -15.0)
@@ -401,193 +430,251 @@ def rank_program(g, core, T, topo):
         dma("sp", "ya%d" % t, T.ya[:, 128 * t:128 * (t + 1)], T["tot%d" % t][:], ["tot%d" % t], [])
 
     def x_rows(t, ph, pl):
-        for f, s in ((4, L("LH", O_N)), (5, L("LL", O_N)), (6, ph), (7, pl)):
-            row("sp", "xr%d" % t, "X", f, s)
+        for f, s in ((4, "nBH"), (5, "nBL"), (6, ph), (7, pl)):
+            row("sp", "xr%d" % t, "X", f, s, ext=[sums_in(t, 3)])
 
     def add_own(t, U):
-        op("pool", lambda: g.dma_start(T[U][:, NW:2 * NW], T[U][:, 0:NW], accum_op=ADD, max_dma_last_dim=4096),
-           [(U, 0, 2 * NW)], [(U, NW, 2 * NW)], grp="vv%d" % t)
+        op("pool", lambda: g.dma_start(T[U][:, NW:NW + UA], T[U][:, 0:UA], accum_op=ADD, max_dma_last_dim=4096),
+           [(U, 0, UA), (U, NW, NW + UA)], [(U, NW, NW + UA)], grp="vv%d" % t, ext=[verdicts_in(t)])
+        dma("sp", "uu%d" % t, T[U][:, NW + UA:2 * NW], T[U][:, UA:NW], [(U, UA, NW)], [(U, NW + UA, 2 * NW)], [verdicts_in(t)])
 
-    def before_verdict0():
-        for k in range(ZM, len(ZS)):
-            make_z(k)
-        gather("act", "X", ("W", 0, NW), "par16", 0, NW)
-        ts("t1", P("p2"), 0.0, EQ)
-        tt("t2", "t1", "n2560", MUL)
+    def nop():
+        pass
+
+    def consts0():
+        ts(("f160", 0, 1), ("fF", 0, 1), 160.0, MUL)
+        ts("nI", "nI", "fF", ADD)
+        digits(O_ITM, NC)
+
+    def consts1():
+        cp(L("LH", O_BIT), L("LI", O_BIT))
+        ts("nzB", "cB", "f160", ADD, 0.0, NE)
+        cp("par16", P("p3"))
+
+    def consts2():
+        ts("t1", P("p2"), 0.0, EQ, 8192.0, MUL)
+        tt("t2", "t1", "n2560", MIN)
         tt("t3", P("p2"), "t2", ADD)
         cp("sc16", "t3")
-        cp("side16", P("p2"))
-        ts(("thb", 0, 1), ("thI", 0, 1), -1.0, MUL, 0.5, ADD)
-        extI("p1", "W", "bit")
+
+    def aconsts0():
+        act("nBH", "nBH", AF.Identity, "f160")
+        act("n2560", "nI", AF.Identity, float(NW))
+        act("oneB", "cB", AF.Identity, 1.0, 0.0)
+
+    def aconsts1():
+        act("nIL", "cB", AF.Identity, "fF", 0.0)
+
+    def late_rows():
+        for f, s in ((R_N, "nBH"), (R_N + 1, "nBL"), (R_ITM, L("LH", O_ITM)), (R_ITM + 1, L("LL", O_ITM)), (R_ONE, "oneB"),
+                     (R_BIT, L("LH", O_BIT)), (R_NZ, "nzB")):
+            row("sp", "late", "W", f, s)
+
+    def before_verdict0():
+        make_z("pd", "r", "kp", "drop", "jzm", "jzp")
+        asel("npre", T.npre[:], "n2560", T.n2560[:], [[-1, NC]], GE_, 0.0, UA // 16 - 1, 0)
+        extI("p1", "W", "sb0")
         extI("p0", "W", "i2b", 0, NW, True, False)
-        extI("p3", "W", "bm", 0, NW, True, False)
-        extI("p7", "X", "itm")
+        gather("act", "X", ("W", 0, NW), "par16", 0, NW)
+        for j, (a, b) in enumerate(TAIL):
+            l = ("sc16", a // 16, b // 16)
+            op("dve", lambda l=l, a=a, b=b: g.vector.tensor_copy(T.SW[:].indirect(ap(l)), T.W[:, a:b]),
+               [l, ("W", a, b)], ["SW"])
+            if j == 0:
+                cp("side16", P("p1"))
+                ts("bitI", P("p1"), 0.0, LT)
+                ts(("thb", 0, 1), ("thI", 0, 1), -1.0, MUL, 0.5, ADD)
+                ts(("fH", 0, 1), ("pI", 0, 1), 10, AND)
+                ts(("dcol", 0, 1), ("fH", 0, 1), 2.0, EQ)
+                ts(("scol", 0, 1), ("dcol", 0, 1), -2.0, MUL, 1.0, ADD)
         x_rows(0, L("LH", O_PAR), L("LL", O_PAR))
-        for h in range(2):
-            l = ("sc16", h * 80, (h + 1) * 80)
-            op("dve", lambda l=l, h=h: g.vector.tensor_copy(T.SW[:].indirect(ap(l)), T.W[:, h * H:(h + 1) * H]),
-               [l, ("W", h * H, (h + 1) * H)], ["SW"])
         gather("act", "SG", ("W", 0, NW), "side16", 0, H)
-        act("sideI", P("p2"))
-        act("bitI", P("p1"))
-        for tt_ in range(2):
-            act(("KW%d" % tt_, NI, NI + 1), ("dcol", 0, 1), AF.Copy)
 
     def after_verdict0():
+        make_z("js", "jn", "sb1", "i2bn", "sg1", "a1")
+        for t in range(2):
+            act(("KW%d" % t, NI, NI + 1), ("dcol", 0, 1), AF.Copy)
         gather("act", "SG", ("W", 0, NW), "side16", H, NW)
-        cp("ip16", P("p7"))
-        for h in range(2):
-            extI("p0", "SG", "sg0", h * H, (h + 1) * H, False, h == 1)
-            extB("p1", "SG", "side", 8 * h, 8 * h + 8, h == 0, h == 1)
+        act("sA0", P("p1"), AF.Relu)
+        act("nbI", "bitI", AF.Identity, 1.0, -1.0)
+        ms(("Ub", NW, NW + 16), 0.0)
+        mm(P("p3"), "M2", "bitI", True, False)
+        mm(P("p6"), "NId", L("LH", O_SIDE), True, False)
+        mm(P("p6"), "NId", L("LL", O_SIDE), False, False)
+        extI("p0", "SG", "sg0", 0, H, False, False)
+        extI("p2", "X", "itm")
+        extI("p0", "SG", "sg0", H, NW, False, True)
         extI("p3", "SW", "a0", 0, NW, False, True)
-        extI("p7", "SW", "n")
-        extB("p6", "SW", "n")
-        act("nbB", L("LF", O_BIT), AF.Identity, 1.0, -1.0)
+        cp("ip16", P("p2"))
+        gather("act", "Ua", ("Ua", 0, NW), "par16", 0, UA // 2, shift=NW)
         act("kaT", P("p0"), AF.Identity, -1024.0)
-        gather("act", "Ua", ("Ua", 0, NW), "par16", 0, NW, shift=NW)
+        gather("act", "Ua", ("Ua", 0, NW), "par16", UA // 2, UA, shift=NW)
         add_own(0, "Ua")
-        tt("sA1", "bitI", "sideI", MUL)
-        tt("sA0", "sideI", "sA1", SUB)
-        tt("t1", P("p1"), "nbB", MUL)
-        tt("t3", "t1", L("LF", O_SIDE), SUB)
-        digits("SH", "SL", "t3")
+        extI("p7", "SW", "n")
+        extB("p6", "SG", "side", 0, 16, False, True)
         tt("t2", P("p3"), "kaT", MIN)
         ts("ka16", "t2", 3072.0, ADD, 1024.0, MIN)
+
+    def late_lists0():
         tt("bpI", P("p7"), "bitI", MUL)
-        cp("predI", P("p7"))
-        tt("t3", "bpI", "sA0", ADD)
-        cp("pt16", "t3")
-        tt("eB", P("p6"), L("LF", O_N), SUB)
-        tt("D0", "eB", L("LF", O_BIT), MUL)
-        digits("DH", "DL", "D0")
+        tt("t3", P("p7"), "nI", SUB)
+        mm(P("p4"), "IDf", "sA0", True, False)
+        mm(P("p4"), "IDf", "bpI", False, True)
+
+    def late_lists1():
+        act("DH", "t3", AF.Copy)
+        act("SH", P("p6"), AF.Copy)
+        cp("pt16", P("p4"))
+        tt("DL", "t3", "DH", SUB)
+
+    def w_half(bank, z, h):
+        return lambda: extI(bank, "W", z, HALF[h][0], HALF[h][1])
+
+    def lists1a():
+        cp("par16", P("p2"))
+        tt("t1", "predI", "bpI", SUB)
+
+    def lists1b():
+        tt("t2", "t1", "sA1", ADD)
+        cp("pt16", "t2")
+
+    def par_digits():
+        cp("pJ", "pB")
+        ts("pK", "pJ", 0xFF0, AND)
+        cp("qH", "pK")
+        tt("qL", "pJ", "pK", SUB)
+
+    def par_rows():
+        row("sp", "pr1", "W", R_PAR, "qH")
+        row("sp", "pr1", "W", R_PAR + 1, "qL")
 
     def before_verdict1():
-        row("sp", "pr1", "W", R_PAR, "pH")
-        row("sp", "pr1", "W", R_PAR + 1, "pL")
-        extI("p1", "C", "n", 0, NW, True, False)
-        mm(P("p1"), "IDf", "P8I", False, True)
-        cp("par16", P("p1"))
-        gather("act", "C", ("W", 0, NW), "pred16", 0, NW)
-        extI("p3", "W", "bp", 0, NW, True, False)
-        extI("p3", "SW", "a1", 0, NW, False, True)
+        gather("act", "C", ("W", 0, NW), "pt16", 0, NW)
+        extI("p2", "W", "i2bn", 0, NW, True, False)
         gather("dve", "X", ("W", 0, NW), "par16", 0, NW)
-        gather("dve", "Uc", ("Uc", 0, NW), "par16", 0, NW, shift=NW)
+        x_rows(1, "pH", "pL")
+        gather("dve", "Uc", ("Uc", 0, NW), "par16", 0, UA, shift=NW)
 
     def after_verdict1():
         add_own(1, "Uc")
+        extI("p1", "C", "side")
+        extI("p2", "C", "sg1", 0, NW, False, True)
         extI("p7", "X", "itm")
-        x_rows(1, "pH", "pL")
-        extI("p2", "C", "side")
-        extI("p0", "W", "i2bn", 0, NW, True, False)
-        extI("p0", "SG", "sg1", 0, NW, False, True)
+        mm(P("p3"), "M2", "nbI", True, False)
+        extI("p3", "C", "a1", 0, NW, False, False)
+        ts("z0", P("p1"), 0.0, EQ, 1024.0, MUL)
+        mm(P("p3"), "IDb", "z0", False, True)
         cp("ip16", P("p7"))
-        tt("t1", "predI", "bpI", SUB)
-        tt("t3", "eB", "D0", SUB)
-        tt("t2", "t1", "sA1", ADD)
-        digits("DH", "DL", "t3")
-        cp("pt16", "t2")
-        tt("t2", P("p2"), "nI", NE)
-        ts("t1", "mI", 1024.0, MUL, 3072.0, ADD)
-        ts("t3", "t2", 1024.0, MUL, 1024.0, ADD)
-        tt("kaT", P("p0"), "t1", ADD)
-        tt("t1", P("p3"), "t3", ADD)
-        tt("t2", "t1", "kaT", MIN)
-        ts("ka16", "t2", 1024.0, MIN)
+        act("kaT", P("p2"))
+        tt("t2", P("p3"), "kaT", MIN)
+        ts("ka16", "t2", 3072.0, ADD, 1024.0, MIN)
 
     def splice_merge(t, U, U1, U2):
         kw = ("KW%d" % t, 0, NI + 1)
-        arr = [("ag%d" % t, sum(len(topo.engines(T.cores[r], core)) for r in range(N) if r != rank))]
+        arr = [verdicts_in(t)]
         bank = ["p0", "p1"]
-        half = [(0, H), (H, NW)]
 
         def cvt(lst, h):
             cp((lst, 80 * h, 80 * (h + 1)), P(bank[h], 80))
-
-        def copy1(j):
-            a, b = TAIL[j]
-            dma("sp", "ud%d_%d" % (t, j), T.Ud[:, a:b], T[U1][:, a:b], [(U1, a, b)], [("Ud", a, b)])
-        mm(P("p5"), "IDf", "n2560", True, False)
-        mm(P("p2"), "IDb", "zB", True, False)
+        mm(P("p5"), "IDf", "npre", True, False)
+        mm(P("p2"), "IDf", "sA%d" % t, True, False)
         for h in range(2):
-            gather("dve", "A", kw, "ip16", half[h][0], half[h][1], "X", MUL, ext=arr)
-            extI(bank[h], "A", "r", half[h][0], half[h][1], o=0)
-            extI("p5", "A", "kp", half[h][0], half[h][1], False, h == 1)
+            a, b = HALF[h]
+            gather("dve", "A", kw, "ip16", a, b, "X", MUL, ext=arr)
+            extI(bank[h], "A", "r", a, b, o=0)
+            extI("p5", "A", "kp", a, min(b, UA), False, False)
+            if h == 0 and t == 0:
+                late_lists0()
         gather("act", "KA", kw, "ka16", 0, NW, ext=arr)
+        if t == 0:
+            late_lists1()
         cvt("j1", 0)
         chain = [("B", "A", "j1", "j2"), ("A", "B", "j2", "j4l"), ("B", "A", "j4l", None)]
         for lv, (o, win, lst, nxt) in enumerate(chain):
             for h in range(2):
-                a, b = half[h]
+                a, b = HALF[h]
                 gather("act", o, win, lst, a, a + SPLIT)
                 gather("dve", o, win, lst, a + SPLIT, b)
                 if h == 0:
                     cvt(lst, 1)
-                if nxt:
-                    extI(bank[h], o, "r", a, b, o=0)
-                    if lv == 0:
-                        extB("p3", "KA", "drop", 8 * h, 8 * h + 8, h == 0, False)
-                    else:
-                        extI("p2", "KA", "drop", a, b, False, False)
-                else:
-                    extB("p4", o, "j", 8 * h, 8 * h + 8, h == 0, h == 1)
-                    extI("p6", o, "j", a, b)
+                extI(bank[h] if nxt else "p2", o, "r" if nxt else "jzm", a, b, nxt is not None, nxt is not None,
+                     0 if nxt else None)
+                if lv == 0 and h == 0:
+                    extI("p5", "A", "pd", UA, NW, False, True)
+                if h == 0 and lv > 0:
+                    extI("p2", "KA", "drop", HALF[lv - 1][0], HALF[lv - 1][1], False, False)
             if nxt:
                 cvt(nxt, 0)
-            if lv == 0:
+            if lv == 1:
                 cp("pe16", P("p5"))
+        row("sp", "rp%d" % t, "A", 0, "nIH")
+        row("sp", "rp%d" % t, "A", 1, "nIL")
         for h in range(2):
-            a, b = half[h]
+            a, b = HALF[h]
             gather("act", "C", "B", "pt16", a, a + PSPLIT)
             gather("dve", "C", "B", "pt16", a + PSPLIT, b)
-            extB("p3", "C", "j", 8 * h, 8 * h + 8, False, h == 1)
-        extI("p2", "C", "j", 0, NW, False, True)
-        for a, b in TAIL:
-            gather("act", U1, U, "pe16", a, b)
-        copy1(0)
-        cp("P8B", P("p4"))
-        cp("P8I", P("p6"))
-        cp("p816", P("p6"))
-        tt("mB", P("p3"), "P8B", EQ)
-        tt("dH", "mB", "DH", MUL)
-        row("sp", "rp%d" % t, "A", R_N, "dH")
-        tt("dL", "mB", "DL", MUL)
-        row("sp", "rp%d" % t, "A", R_N + 1, "dL")
-        copy1(1)
+            extI("p2", "C", "jzp", a, b, False, h == 1)
+        extI("p1", "B", "js")
+        def spliced(j):
+            a, b = PIECE[j]
+            if a < UA:
+                gather("act", U1, (U, 0, NW + UA), "pe16", a, b)
+            else:
+                gather("dve", U1, (U, 0, NW), "pe16", a, b, U, ADD, shift1=NW)
+            return lambda: dma("sp", "ud%d_%d" % (t, j), T.Ud[:, a:b], T[U1][:, a:b], [(U1, a, b)], [("Ud", a, b)])
+        spliced(0)()
+        spliced(1)
+        ts("mI", P("p2"), 0.0, EQ)
+        tt("dH", "mI", "DH", MUL)
+        row("sp", "rp%d" % t, "A", 2, "dH")
+        tt("dL", "mI", "DL", MUL)
+        row("sp", "rp%d" % t, "A", 3, "dL")
+        ts("se16", P("p2"), float(NW), MIN, 0.0, MAX)
+        spliced(2)()
+        spliced(3)()
+        act(("Ud",) + PIECE[1], (U1,) + PIECE[1], AF.Copy)
+        cp("p816", P("p1"))
         if t == 0:
-            tt("sH", "mB", "SH", MUL)
-            row("sp", "sd1", "W", R_DS, "sH")
-            tt("sL", "mB", "SL", MUL)
-            row("sp", "sd1", "W", R_DS + 1, "sL")
-        copy1(2)
-        copy1(3)
-        tt("mI", P("p2"), "P8I", EQ)
-        tt("t1", "mI", "sA%d" % t, MUL)
-        cp("se16", "t1")
-        mm(P("p3"), "IDf", "P8B", True, False)
+            tt("SL", P("p6"), "SH", SUB)
+            act("predI", P("p7"))
+            extB("p3", "KA", "drop", 0, 16, True, False)
+            extB("p3", "B", "jzm", 0, 16, False, False)
+            extB("p3", "C", "jzp", 0, 16, False, True)
         for j, (a, b) in enumerate(TAIL):
-            gather("act", "C", "A", "p816", a, b)
-            gather("dve", U2, U1, "se16", a, b, "Ud", ADD)
-            extB("p3", "C", "n", a // NC, b // NC, False, b == NW)
+            gather("act", "SG", "A", "p816", a, b)
+            gather("dve", U2, (U1, 0, NW + 1), "se16", PIECE[j][0], PIECE[j][1], "Ud", ADD)
+            if t == 0 and j == 3:
+                ge4(U2, 0, 960, True)
+            extB("p4", "SG", "jn", a // NC, b // NC, a == 0, b == NW)
             if t == 1:
+                a, b = PIECE[j]
                 ts(("Y", a, b), (U2, a, b), 15.0, MIN)
                 dma("sp", "yc%d" % j, T.yc[:, a:b], T.Y[:, a:b], [("Y", a, b)], [])
         if t == 0:
-            ge4(U2, 800, 1760, True)
-            ge4(U2, 0, 800, False, "act")
-            ge4(U2, 1760, NW, False)
-            digits("pH", "pL", P("p3"))
+            ge4(U2, 960, 1920, False)
+            ge4(U2, 1920, NW, False)
+            act("pH", P("p4"), AF.Copy)
+            act(("Y", 9 * NC, NW), (U2, 9 * NC, NW), AF.Relu, 15.0, -1.0)
+            ts("mB", P("p3"), 0.0, EQ)
+            for f, o, d in ((R_DS, "sH", "SH"), (R_DS + 1, "sL", "SL")):
+                tt(o, "mB", d, MUL)
+                row("sp", "sd1", "W", f, o)
+            tt("pL", P("p4"), "pH", SUB)
+            act("pB", P("p4"))
         else:
-            act("ypB", P("p3"))
+            act("ypB", P("p4"))
             dma("act", "yp0", T.yp[:], T.ypB[:], ["ypB"], [])
 
     prep(0, "Ua")
-    walks(0)
+    walks(0, [lambda: extI("p3", "W", "par"), w_half("p2", "side", 0), w_half("p2", "side", 1), nop],
+          [consts0, consts1, consts2], [aconsts0, aconsts1, nop], late_rows, nop)
     before_verdict0()
     verdict(0)
     after_verdict0()
     splice_merge(0, "Ua", "Ub", "Uc")
     prep(1, "Uc")
-    walks(1)
+    walks(1, [lambda: extI("p2", "SG", "jn"), w_half("p3", "sb1", 0), w_half("p3", "sb1", 1), nop], [par_digits, lists1a, nop],
+          [nop, nop, lambda: act("sA1", P("p3"), AF.Relu, -4096.0)], par_rows, lists1b)
     before_verdict1()
     verdict(1)
     after_verdict1()

@@ -3,7 +3,9 @@ from concourse.mybir import AluOpType, ActivationFunctionType
 
 NW, NI, NC = 2560, 1024, 160
 H = NW // 2
-R_N, R_PAR, R_PU, R_SIDE, R_ITM, R_DS, R_ONE, R_UP, R_BIT, R_NZ = 0, 2, 4, 6, 8, 10, 12, 13, 14, 15
+R_N, R_PAR, R_PU, R_SIDE, R_ITM, R_DS, R_ONE, R_UP, R_BIT = 0, 2, 4, 6, 8, 10, 12, 13, 14
+R_NZ = R_ONE
+BIG = 2.0 ** 22
 
 
 def pair(r, w=1.0):
@@ -19,14 +21,13 @@ ZS = [
     ("n", None, pair(R_N)),
     ("side", None, {R_SIDE: 1.0, R_SIDE + 1: 1.0, R_DS: 1.0, R_DS + 1: 1.0}),
     ("x", "side", {R_UP: 4096.0}),
-    ("lin0", "side", pair(R_PU)),
-    ("lin", "lin0", {R_UP: 2560.0}),
+    ("lin", "side", {R_PU: 1.0, R_PU + 1: 1.0, R_UP: 2560.0}),
     ("par", None, pair(R_PAR)),
     ("sb0", "side", {R_BIT: -4096.0}),
     ("itm", None, pair(R_ITM)),
     ("i2b", "itm", {R_BIT: 2048.0}),
     ("sg0", None, {R_BIT: -1024.0, R_NZ: -1024.0}),
-    ("a0", "itm", {R_BIT: 1024.0, R_ONE: -1024.0}),
+    ("a0", "itm", {R_BIT: 1024.0, R_ONE: -4096.0}),
     ("pd", None, pair(6)),
     ("r", "pd", pair(4)),
     ("kp", None, {R_ONE: -2560.0}),
@@ -38,18 +39,20 @@ ZS = [
     ("sb1", "side", {R_BIT: 4096.0}),
     ("i2bn", "itm", {R_BIT: -2048.0}),
     ("sg1", None, {R_BIT: 1024.0, R_NZ: -1024.0}),
-    ("a1", "itm", {R_BIT: -1024.0}),
+    ("a1", "itm", {R_BIT: -BIG, R_NZ: -BIG, R_DS: -1024.0, R_DS + 1: -1024.0}),
 ]
 ZI = {z[0]: k for k, z in enumerate(ZS)}
-ZE = 7
+ZE = 6
+ZM = 11
+ZL = 19
 ZW = 144
 UA = 1600
 
 SCRATCH = {}
-for _n in ("A", "B", "C", "KA", "GE", "Y", "UM", "SG", "X", "Ud"):
+for _n in ("A", "B", "C", "KA", "Y", "UM", "SG", "X", "Ud"):
     SCRATCH[_n] = ("sbuf", [128, NW], "bfloat16")
 SCRATCH["Ub"] = ("sbuf", [128, NW + 16], "bfloat16")
-for _n in ("W", "SW", "Ua", "Uc"):
+for _n in ("W", "GE", "Ua", "Uc"):
     SCRATCH[_n] = ("sbuf", [128, 2 * NW], "bfloat16")
 for _n in ("F0", "F1", "G0", "G1", "G2", "S", "ACC0", "ACC1", "LAND0", "LAND1"):
     SCRATCH[_n] = ("sbuf", [128, NI], "bfloat16")
@@ -57,27 +60,27 @@ for _n in ("KW0", "KW1"):
     SCRATCH[_n] = ("sbuf", [128, NI + 16], "bfloat16")
 SCRATCH["ZZ"] = ("sbuf", [128, len(ZS) * ZW], "bfloat16")
 SCRATCH["BZ"] = ("sbuf", [128, 16 * 128], "bfloat16")
-for _n in ("IDb", "NId", "M2", "BO", "s1", "s2", "c15"):
+for _n in ("IDb", "NId", "M2", "BO", "s1", "c15"):
     SCRATCH[_n] = ("sbuf", [128, 128], "bfloat16")
-for _n in ("IDf", "tot0", "tot1"):
+for _n in ("IDf", "tot"):
     SCRATCH[_n] = ("sbuf", [128, 128], "float32")
 O_HEAD, O_PAR, O_SIDE, O_ITM, O_BIT, O_END = 0, 64, 224, 384, 544, 704
 for _n in ("LI", "HI"):
     SCRATCH[_n] = ("sbuf", [128, O_END], "int32")
 for _n in ("LH", "LL"):
     SCRATCH[_n] = ("sbuf", [128, O_END], "bfloat16")
-for _n in ("nI", "n2560", "npre", "predI", "sA0", "sA1", "t1", "t2", "t3", "ypB", "kaT", "bpI", "pB"):
+for _n in ("nI", "n2560", "npre", "predI", "sA0", "sA1", "t1", "t2", "t3", "kaT", "bpI", "pB"):
     SCRATCH[_n] = ("sbuf", [128, NC], "float32")
 for _n in ("pJ", "pK"):
     SCRATCH[_n] = ("sbuf", [128, NC], "int32")
-for _n in ("upB", "puH", "puL", "dH", "dL", "sH", "sL", "pH", "pL", "qH", "qL", "DH", "DL", "mB", "mI", "SH", "SL", "bitI",
-           "nbI", "z0", "nBH", "nBL", "nIH", "nIL", "cB", "nzB", "oneB"):
+for _n in ("upB", "puH", "puL", "eH", "eL", "euH", "euL", "dH", "dL", "sH", "sL", "pH", "pL", "qH", "qL", "DH", "DL", "mB", "mI", "SH", "SL", "bitI",
+           "nbI", "nBH", "nBL", "nIH", "nIL", "cB", "nzB", "oneB"):
     SCRATCH[_n] = ("sbuf", [128, NC], "bfloat16")
 for _n in ("par16", "side16", "ip16", "sc16", "ka16", "pt16", "j1", "j2", "j4l", "pe16", "p816", "se16"):
     SCRATCH[_n] = ("sbuf", [128, NC], "uint16")
 for _n in ("hd16", "ix1", "ix2", "w1", "w2", "w3"):
     SCRATCH[_n] = ("sbuf", [128, 64], "uint16")
-for _n in ("k0", "k1", "k2", "wa", "wb", "wu"):
+for _n in ("k0", "k1", "wa", "wb", "wu"):
     SCRATCH[_n] = ("sbuf", [128, 64], "float32")
 for _n in ("thI", "pI", "fI", "fH"):
     SCRATCH[_n] = ("sbuf", [128, 4], "int32")
@@ -91,7 +94,7 @@ for _k in range(8):
 ENG = ["pe", "dve", "act", "pool"]
 DMAG = ["ldh", "ldp", "ldi", "ldu0", "ldu1", "ldu2", "ldu3", "ldth", "hd0", "late", "swz", "fw0", "fx0", "fw1", "fx1", "rp0", "rp1",
         "sd1", "pr1", "vv0", "vv1", "xr0", "xr1", "ya0", "ya1", "yc0", "yc1", "yc2", "yc3", "yp0", "uu0", "uu1"] + \
-    ["ud%d_%d" % (_t, _j) for _t in range(2) for _j in (0, 2, 3)]
+    ["ud%d_%d" % (_t, _j) for _t in range(2) for _j in (1, 3)]
 SEMAPHORES = ["e_" + _e for _e in ENG] + ["d_" + _d for _d in DMAG] + ["sent"] + \
     ["rs%d_%d" % (_t, _m) for _t in range(2) for _m in range(4)] + ["ag0", "ag1"]
 
@@ -99,12 +102,17 @@ ADD, SUB, MUL, MAX, MIN = AluOpType.add, AluOpType.subtract, AluOpType.mult, Alu
 GE_, LT, EQ, NE = AluOpType.is_ge, AluOpType.is_lt, AluOpType.is_equal, AluOpType.not_equal
 AND = AluOpType.bitwise_and
 AF = ActivationFunctionType
-SPLIT = 672
-PSPLIT = 640
-CUT = ((768, 768, 768), (704, 704, 640))
+FIRST = 448
+PART = [(0, 896), (896, 1792), (1792, NW)]
+SPLIT = (512, 480, 416)
+CUT = ((704, 768, 640), (640, 704, 576))
+FILL = ((2, 2, 1), (1, 1, 0))
+PAIRS = (2, 3, 1, 0)
 TAIL = [(640 * _j, 640 * (_j + 1)) for _j in range(4)]
 HALF = [(0, H), (H, NW)]
-PIECE = [(UA, 2080), (0, 800), (2080, NW), (800, UA)]
+LOAD = [(0, 800), (800, 1600), (1600, 2240), (2240, NW)]
+PIECE = [(0, 800), (800, UA), (UA, 2080), (2080, NW)]
+LAST = (2, 0, 3, 1)
 
 
 def rank_program(g, core, T, topo):
@@ -197,7 +205,7 @@ def rank_program(g, core, T, topo):
         op("pe", fn, [(src, NC * i0, NC * i1), zreg(z)], [bank])
 
     def spread(bank, src, i0, i1, lhs=None, win=None):
-        if win:
+        if lhs:
             mm(P(bank, NC * (i1 - i0)), lhs, (win, NC * i0, NC * i1), True, False)
 
         def fn():
@@ -209,6 +217,10 @@ def rank_program(g, core, T, topo):
 
     def mm(o, lhs, rhs, start, stop, ext=()):
         op("pe", lambda: g.tensor.matmul(ap(o), T[lhs][:], ap(rhs), start, stop), [lhs, rhs], [o], ext=ext)
+
+    def add_up(bank, terms, start=True, stop=True):
+        for j, (lhs, x) in enumerate(terms):
+            mm(P(bank), lhs, x, start and j == 0, stop and j == len(terms) - 1)
 
     def dma(q, grp, out, in_, r, w, ext=()):
         op(q, lambda: Q[q].dma_start(out, in_), r, w, grp=grp, ext=ext)
@@ -250,16 +262,12 @@ def rank_program(g, core, T, topo):
 
     def make_z(*names):
         view = lambda z: T.ZZ[:, ZI[z] * ZW + 16:(ZI[z] + 1) * ZW:16]
-        for name in names:
-            _, base, wts = ZS[ZI[name]]
-            if wts is None:
-                asel("z8", T.z8[:], "IDb", T.IDb[:, 0:8], [[-16, 8]], GE_, 0.0, 0, 1)
-                asel(zreg(name), view(name), "z8", T.z8[:], [[16, 8]], GE_, 0.0, 15, -1)
-            else:
-                src = base or name
-                for f in sorted(wts):
+        for j in range(4):
+            for name in names:
+                _, base, wts = ZS[ZI[name]]
+                if j < len(wts):
+                    f, src = sorted(wts)[j], name if j else base or name
                     asel(zreg(name), view(name), zreg(src), view(src), [[-16, 8]], NE, wts[f], -f, 1)
-                    src = name
 
     def zero(o, i):
         act(o, i, AF.Identity, 0.0, 0.0)
@@ -270,134 +278,198 @@ def rank_program(g, core, T, topo):
     load("sp", "ldh", "heads", O_HEAD, 64)
     load("act", "ldp", "par", O_PAR, NC)
     load("sp", "ldp", "side", O_SIDE, NC)
-    for j, (a, b) in enumerate(TAIL):
-        dma("act" if j % 2 == 0 else "sp", "ldu%d" % j, T.Ua[:, a:b], T.cnt[:, a:b], [], [("Ua", a, b)])
-    load("sp", "ldi", "itm", O_ITM, NC)
-    load("sp", "ldi", "bit", O_BIT, NC)
+    for j, (a, b) in enumerate(LOAD):
+        dma("sp", "ldu%d" % j, T.Ua[:, a:b], T.cnt[:, a:b], [], [("Ua", a, b)])
     iota(("pI", 0, 1), [[0, 1]], 1, False)
     iota("OH", [[1, 16]])
     ms("c15", 15.0)
     ms("IDb", 1.0)
+    ts(("fH", 0, 1), ("pI", 0, 1), 10, AND)
     ms(("ZZ", 0, ZE * ZW), 0.0)
-    ms(("W", NW, NW + H), 0.0)
+    ts(("dcol", 0, 1), ("fH", 0, 1), 2.0, EQ)
     ts(("fI", 0, 1), ("pI", 0, 1), 15, AND)
+    ms(("W", NW, NW + H), 0.0)
+    ts(("scol", 1, 2), ("dcol", 0, 1), 240.0, MUL, -120.0, ADD)
     cp(("fF", 0, 1), ("fI", 0, 1))
-    ts("OH", "OH", "fF", EQ)
     ms(("W", 0, NW), 0.0)
+    ts("OH", "OH", "fF", EQ)
     asel("BO", T.BO[:], "c15", T.c15[:], [[-16, 8], [0, 16]], GE_, 0.0, 0, 1)
+    asel("z8", T.z8[:], "IDb", T.IDb[:, 0:8], [[-16, 8]], GE_, 0.0, 0, 1)
     asel("BO", T.BO[:], "BO", T.BO[:], [[16, 8], [0, 16]], GE_, 0.0, 15, -1)
-    make_z("all", "par")
-    act(("W", NW + H, 2 * NW), ("W", NW, NW + H), AF.Copy)
-    for i in range(10):
-        act(("BZ", 128 * i, 128 * (i + 1)), "BO", AF.Identity, 0.0, ("OH", i, i + 1))
+    asel(zreg("all"), T.ZZ[:, 16:ZW:16], "z8", T.z8[:], [[16, 8]], GE_, 0.0, 15, -1)
     asel("IDb", T.IDb[:], "IDb", T.IDb[:], [[-1, 128]], EQ, 0.0, 0, 1)
-    for i in range(10, 16):
+    act(("W", NW + H, 2 * NW), ("W", NW, NW + H), AF.Copy)
+    act("NId", "IDb", AF.Identity, 0.0, -1.0)
+
+    def spreader(i):
+        act(("BZ", 128 * i, 128 * (i + 1)), "BO", AF.Identity, 0.0, ("OH", i, i + 1))
+    for i in range(9):
+        if i == 6:
+            make_z("par", "side")
         z = ("BZ", 128 * i, 128 * (i + 1))
         asel(z, ap(z), "c15", T.c15[:], [[-16, 8], [0, 16]], EQ, 0.0, -i, 1)
-    make_z("side", "x", "lin0", "lin")
+    make_z("lin", "x")
     iota("nI", [[16, NC]])
     iota("cB", [[1, NC]])
     iota("nBL", [[0, 10], [1, 16]])
     iota("nBH", [[16, 10], [0, 16]])
     iota("nIH", [[16, NC]])
     op("pool", lambda: g.dma_start(T.thI[:, 0:1], T.th[:], allow_slow_non_contiguous=True), [], [("thI", 0, 1)], grp="ldth")
-    iota(("ZZ", ZE * ZW, len(ZS) * ZW), [[0, (len(ZS) - ZE) * ZW]])
-    make_z("n", "sb0", "itm", "i2b", "sg0", "a0")
-    digits(O_HEAD, 64)
+    parts = ((O_HEAD, 64), (O_PAR, 2 * NC))
+    for o, n in parts:
+        ts(L("HI", o, n), L("LI", o, n), 0xFF0, AND)
+    for o, n in parts:
+        cp(L("LH", o, n), L("HI", o, n))
+        tt(L("LL", o, n), L("LI", o, n), L("HI", o, n), SUB)
     row("sp", "hd0", "W", R_PAR, L("LH", O_HEAD, 64), NW, NI)
     row("sp", "hd0", "W", R_PAR + 1, L("LL", O_HEAD, 64), NW, NI)
-    digits(O_PAR, 2 * NC)
     for f, o in ((R_SIDE, O_SIDE), (R_PAR, O_PAR)):
         row("sp", "fw0", "W", f, L("LH", o))
         row("sp", "fw0", "W", f + 1, L("LL", o))
 
-    def ge4(U, a, b, first, eng="dve"):
+    def ge4(U, a, b, first, eng="dve", last=False):
         if eng == "dve":
             ts(("GE", a, b), (U, a, b), 4.0, GE_, 0.5, SUB)
         else:
             act(("GE", a, b), (U, a, b), AF.Sign, -3.5)
-        extB("p0", "GE", "all", a // NC, b // NC, first, b == NW)
+        extB("p0", "GE", "all", a // NC, b // NC, first, last)
+
+    def nop():
+        pass
 
     def prep(t, U):
         if t == 0:
-            for j, (a, b) in enumerate(TAIL):
-                ge4(U, a, b, a == 0, "act" if j == 1 else "dve")
-            extI("p1", "W", "par", NW, NW + NI, o=0)
+            add_up("p4", (("IDb", L("LH", O_PAR)), ("IDb", L("LL", O_PAR)), ("NId", L("LH", O_SIDE)),
+                          ("NId", L("LL", O_SIDE))))
+            for j, (a, b) in enumerate(LOAD):
+                ge4(U, a, b, j == 0, "act" if j == 0 else "dve", j == 3)
+                if j == 0:
+                    for k in ("KW0", "KW1"):
+                        act((k, NI, NI + 1), ("scol", 1, 2), AF.Sigmoid)
+                    act("eH", P("p4"), AF.Copy)
+                    for i in range(9, 16):
+                        spreader(i)
+                if j == 3:
+                    tt("eL", P("p4"), "eH", SUB)
+                    ts(("scol", 0, 1), ("dcol", 0, 1), -16.0, MUL, 8.0, ADD)
+                    ms(("Ub", NW, NW + 16), 0.0)
+                    ts(("f160", 0, 1), ("fF", 0, 1), 160.0, MUL)
             ph, pl = L("LH", O_PAR), L("LL", O_PAR)
         else:
             ph, pl = "pH", "pL"
+        lhs, win = ("NId", "Y") if t else ("IDb", U)
+        mm(P("p6", 3 * NC), lhs, (win, 13 * NC, 16 * NC), True, False)
+        mm(P("p7", 2 * NC), lhs, (win, 11 * NC, 13 * NC), True, False)
         ts("upB", P("p0"), 0.5, GE_)
         row("sp", "fw%d" % t, "W", R_UP, "upB")
-        tt("puH", ph, "upB", MUL)
-        row("sp", "fw%d" % t, "W", R_PU, "puH")
-        tt("puL", pl, "upB", MUL)
-        row("sp", "fw%d" % t, "W", R_PU + 1, "puL")
-        for f, s in ((R_UP, "upB"), (R_PU, "puH"), (R_PU + 1, "puL")):
-            row("sp", "fx%d" % t, "W", f, s, NW)
         if t == 0:
+            ms("mI", 0.0)
+        else:
+            tt("eL", P("p4"), "eH", SUB)
+        tt("euH", "eH", "upB", MUL)
+        row("sp", "fw%d" % t, "W", R_PU, "euH")
+        tt("euL", "eL", "upB", MUL)
+        row("sp", "fw%d" % t, "W", R_PU + 1, "euL")
+        if t == 0:
+            extI("p1", "W", "par", NW, NW + NI, o=0)
             cp("hd16", P("p1", 64))
+
+        def second_half():
+            if t == 1:
+                tt("pL", P("p3"), "pH", SUB)
+                act("pB", P("p3"))
+            tt("puH", ph, "upB", MUL)
+            tt("puL", pl, "upB", MUL)
+            for f, s in ((R_UP, "upB"), (R_PU, "puH"), (R_PU + 1, "puL")):
+                row("sp", "fx%d" % t, "W", f, s, NW)
+        if t == 0:
             act("IDf", "IDb")
-            act("M2", "IDb", AF.Identity, 0.0, -2048.0)
-            act("NId", "IDb", AF.Identity, 0.0, -1.0)
-            dma("sp", "swz", T.SW[:, 0:NW], T.W[:, NW:2 * NW], [("W", NW, 2 * NW)], [("SW", 0, NW)])
-        for (i0, i1), (k0, k1), b, c in (((0, 3), (9, 12), "p5", "p6"), ((3, 6), (12, 14), "p4", "p7"),
-                                         ((6, 9), (14, 16), "p5", "p6")):
+        for (i0, i1), (k0, k1), b, c in (((0, 3), (13, 16), "p5", "p6"), ((3, 6), (11, 13), "p4", "p7"),
+                                         ((6, 9), (9, 11), "p5", "p6")):
             spread(b, "upB", i0, i1)
             tt(("UM", NC * i0, NC * i1), P(b, NC * (i1 - i0)), (U, NC * i0, NC * i1), MIN)
-            spread(c, "upB", k0, k1, "NId" if t else "IDb", "Y" if t else U)
+            spread(c, "upB", k0, k1, lhs if i0 == 6 else None, win)
             act(("UM", NC * k0, NC * k1), P(c, NC * (k1 - k0)), AF.Relu, 0.0 if t else -15.0)
+            if i0 == 0 and t == 1:
+                add_up("p3", [("IDb", x) for x in (L("LH", O_SIDE), L("LL", O_SIDE), "sH", "sL", "eH", "eL")])
+                act("pH", P("p3"), AF.Copy)
+            if i0 == 3 * t:
+                second_half()
+        if t == 0:
+            load("sp", "ldi", "itm", O_ITM, NC)
+            load("sp", "ldi", "bit", O_BIT, NC)
+            for f in (R_N, R_N + 1, R_ONE):
+                row("sp", "swz", "GE", f, "mI")
 
-    def walks(t, pe_fill, dve_fill, act_fill, after_f, in_sums):
+    def walks(t, pe_fill, act_fill, spare, after_fields):
         acc = "ACC%d" % t
+
+        def fill(n=1):
+            for _ in range(n):
+                if spare:
+                    spare.pop(0)()
+
         gather("act", "F0", ("W", 0, NW), "hd16", 0, 512)
         gather("dve", "F0", ("W", 0, NW), "hd16", 512, NI)
         pe_fill[0]()
-        lists = ["hd16", "w1", "w2", "w3"]
         for s in range(3):
-            k, F = "k%d" % s, "F%d" % (s % 2)
-            for bank, z in (("p0", "x"), ("p1", "lin" if s < 2 else "lin0")):
-                if s > 0:
-                    mm(P(bank, 64), "IDf", "k%d" % (s - 1), True, False)
-                extI(bank, F, z, 0, NI, s == 0, True)
-            gather("act", "G%d" % s, "UM", lists[s], 0, CUT[t][s])
-            gather("dve", "G%d" % s, "UM", lists[s], CUT[t][s], NI)
-            dve_fill[s]()
-            ts(k, P("p0", 64), -4096.0, ADD, 0.0, MAX)
+            F, w, p = "F%d" % (s % 2), "w%d" % s if s else "hd16", P("p1", 64)
+            extI("p1", F, "lin", 0, NI)
+            if s == 1:
+                mm(P("p0", 64), "IDf", "k0", True, False)
             if s < 2:
-                ts("wu", P("p0", 64), 4096.0, GE_, float(NW), MUL)
-            tt("wa", P("p1", 64), k, SUB)
-            cp("ix%d" % (s + 1) if s < 2 else "w3", "wa")
+                extI("p0", F, "x", 0, NI, s == 0, True)
+            gather("act", "G%d" % s, "UM", w, 0, CUT[t][s])
+            gather("dve", "G%d" % s, "UM", w, CUT[t][s], NI)
             for h in range(2):
                 mm("p%d" % (6 + h), "IDb", ("G%d" % s, 512 * h, 512 * (h + 1)), s == 0, s == 2)
             pe_fill[s + 1]()
-            act_fill[s]()
+            fill(FILL[t][s])
+            if s:
+                tt("wa", p, "k%d" % (s - 1), MAX)
+            else:
+                cp("ix1", p)
+            ts("wu", p, float(NW), GE_, float(NW), MUL)
+            if s == 1:
+                cp("ix2", "wa")
+            if s != 1:
+                fill()
+            tt("wb", "wa" if s else p, "wu", SUB)
             if s < 2:
-                F = "F%d" % ((s + 1) % 2)
-                tt("wb", "wa", "wu", SUB)
-                gather("act", F, "W", "ix%d" % (s + 1), 0, 512)
-                gather("dve", F, "W", "ix%d" % (s + 1), 512, NI)
-                cp(lists[s + 1], "wb")
+                F = "F%d" % (1 - s)
+                act_fill[s]()
+                gather("act", F, "W", "ix%d" % (s + 1), 0, 608)
+                gather("dve", F, "W", "ix%d" % (s + 1), 608, NI)
                 if s == 1:
-                    after_f()
-        order = [(rank // 2 + m) % 4 for m in (1, 2, 3, 0)]
-        for c in order:
-            act(("S", 256 * c, 256 * (c + 1)), ("p%d" % (6 + c // 2), 256 * (c % 2), 256 * (c % 2 + 1)), AF.Copy)
-        for m, c in enumerate(order):
-            gather("dve", acc, "UM", "w3", 256 * c, 256 * (c + 1), "S", ADD)
-            to = [r for r in (2 * c, 2 * c + 1) if r != rank]
+                    after_fields()
+            else:
+                fill()
+            cp("w%d" % (s + 1), "wb")
+            if s < 2:
+                ts("k%d" % s, P("p0", 64), -4096.0, ADD, 0.0, MAX)
+                fill()
 
-            def send(to=to, m=m):
+        def sums(m):
+            c = rank // 2 ^ PAIRS[m]
+            act(("S", 256 * c, 256 * (c + 1)), ("p%d" % (6 + c // 2), 256 * (c % 2), 256 * (c % 2 + 1)), AF.Copy)
+            gather("dve", acc, "UM", "w3", 256 * c, 256 * (c + 1), "S", ADD)
+            to = senders(m)
+
+            def send():
                 tr = [RemoteDMATransfer(dst_ids=[dst(r)], dma_engine_mask=bits(engs(r, j, len(to))),
                                         remote_sem=T.sem["rs%d_%d" % (t, m)], src=T[acc][:, 128 * r:128 * (r + 1)],
                                         dst=T["LAND%d" % t][:, 128 * rank:128 * (rank + 1)]) for j, r in enumerate(to)]
                 return g.remote_dma_fused(tr, local_sem=T.sem.sent)
             sent[0] += sum(len(engs(r, j, len(to))) for j, r in enumerate(to))
             op("pool", send, [(acc, 256 * c, 256 * (c + 1))], [], inc=False)
-            if m == 1:
-                in_sums()
+        for m in range(4):
+            sums(m)
+            if m:
+                fill()
+        fill(len(spare))
 
     def senders(m):
-        c = (rank // 2 - (m + 1)) % 4
+        c = rank // 2 ^ PAIRS[m]
         return [r for r in (2 * c, 2 * c + 1) if r != rank]
 
     def sums_in(t, m):
@@ -415,8 +487,7 @@ def rank_program(g, core, T, topo):
                 mm(P("p4", 128), "IDb", (land, 128 * r, 128 * (r + 1)), False, m == 3, ext=[sums_in(t, m)])
         act("s1", P("p4", 128), AF.Sign, "thb")
         mm(P("p5", 128), "BO", "s1", True, True)
-        act("s2", P("p5", 128), AF.Sign, -15.0)
-        act((kw,) + own, "s2", AF.Relu, 0.0, "scol")
+        act((kw,) + own, P("p5", 128), AF.Sigmoid, ("scol", 1, 2), ("scol", 0, 1))
         oth = [(rank + d) % N for d in range(1, N)]
 
         def send():
@@ -426,8 +497,8 @@ def rank_program(g, core, T, topo):
             return g.remote_dma_fused([tr], local_sem=T.sem.sent)
         sent[0] += len(engs(oth[0], 0, 1))
         op("pool", send, [(kw,) + own], [], inc=False)
-        act("tot%d" % t, P("p4", 128))
-        dma("sp", "ya%d" % t, T.ya[:, 128 * t:128 * (t + 1)], T["tot%d" % t][:], ["tot%d" % t], [])
+        act("tot", P("p4", 128))
+        dma("sp", "ya%d" % t, T.ya[:, 128 * t:128 * (t + 1)], T.tot[:], ["tot"], [], [verdicts_in(t)])
 
     def x_rows(t, ph, pl):
         for f, s in ((4, "nBH"), (5, "nBL"), (6, ph), (7, pl)):
@@ -438,183 +509,203 @@ def rank_program(g, core, T, topo):
            [(U, 0, UA), (U, NW, NW + UA)], [(U, NW, NW + UA)], grp="vv%d" % t, ext=[verdicts_in(t)])
         dma("sp", "uu%d" % t, T[U][:, NW + UA:2 * NW], T[U][:, UA:NW], [(U, UA, NW)], [(U, NW + UA, 2 * NW)], [verdicts_in(t)])
 
-    def nop():
-        pass
+    itm = [L(x, O_ITM) for x in ("LI", "HI", "LH", "LL")]
+    spare0 = [lambda: ts("nI", "nI", "fF", ADD),
+              lambda: ts("nzB", "cB", "f160", ADD, 0.0, NE),
+              lambda: ts(itm[1], itm[0], 0xFF0, AND),
+              lambda: cp(L("LH", O_BIT), L("LI", O_BIT)),
+              lambda: cp(itm[2], itm[1]),
+              lambda: tt(itm[3], itm[0], itm[1], SUB),
+              lambda: cp("par16", P("p3")),
+              lambda: ts("t1", P("p2"), 0.0, EQ, 8192.0, MUL),
+              lambda: tt("t2", "t1", "n2560", MIN),
+              lambda: tt("t3", P("p2"), "t2", ADD),
+              lambda: cp("sc16", "t3")]
 
-    def consts0():
-        ts(("f160", 0, 1), ("fF", 0, 1), 160.0, MUL)
-        ts("nI", "nI", "fF", ADD)
-        digits(O_ITM, NC)
-
-    def consts1():
-        cp(L("LH", O_BIT), L("LI", O_BIT))
-        ts("nzB", "cB", "f160", ADD, 0.0, NE)
-        cp("par16", P("p3"))
-
-    def consts2():
-        ts("t1", P("p2"), 0.0, EQ, 8192.0, MUL)
-        tt("t2", "t1", "n2560", MIN)
-        tt("t3", P("p2"), "t2", ADD)
-        cp("sc16", "t3")
+    def scatter(a, b):
+        l = ("sc16", a // 16, b // 16)
+        op("dve", lambda: g.vector.tensor_copy(T.GE[:].indirect(ap(l)), T.W[:, a:b]), [l, ("W", a, b)], ["GE"])
 
     def aconsts0():
         act("nBH", "nBH", AF.Identity, "f160")
         act("n2560", "nI", AF.Identity, float(NW))
-        act("oneB", "cB", AF.Identity, 1.0, 0.0)
+
+    def selectors():
+        iota(("ZZ", ZE * ZW, ZM * ZW), [[0, (ZM - ZE) * ZW]])
+        make_z("itm", "sb0", "n", "sg0")
+        make_z("a0", "i2b")
 
     def aconsts1():
         act("nIL", "cB", AF.Identity, "fF", 0.0)
+        act("M2", "IDb", AF.Identity, 0.0, -2048.0)
 
     def late_rows():
-        for f, s in ((R_N, "nBH"), (R_N + 1, "nBL"), (R_ITM, L("LH", O_ITM)), (R_ITM + 1, L("LL", O_ITM)), (R_ONE, "oneB"),
-                     (R_BIT, L("LH", O_BIT)), (R_NZ, "nzB")):
+        for f, s in ((R_N, "nBH"), (R_N + 1, "nBL"), (R_ITM, L("LH", O_ITM)), (R_ITM + 1, L("LL", O_ITM)), (R_ONE, "nzB"),
+                     (R_BIT, L("LH", O_BIT))):
             row("sp", "late", "W", f, s)
 
     def before_verdict0():
-        make_z("pd", "r", "kp", "drop", "jzm", "jzp")
-        asel("npre", T.npre[:], "n2560", T.n2560[:], [[-1, NC]], GE_, 0.0, UA // 16 - 1, 0)
+        iota(("ZZ", ZM * ZW, ZL * ZW), [[0, (ZL - ZM) * ZW]])
         extI("p1", "W", "sb0")
         extI("p0", "W", "i2b", 0, NW, True, False)
+        aconsts1()
         gather("act", "X", ("W", 0, NW), "par16", 0, NW)
-        for j, (a, b) in enumerate(TAIL):
-            l = ("sc16", a // 16, b // 16)
-            op("dve", lambda l=l, a=a, b=b: g.vector.tensor_copy(T.SW[:].indirect(ap(l)), T.W[:, a:b]),
-               [l, ("W", a, b)], ["SW"])
-            if j == 0:
-                cp("side16", P("p1"))
-                ts("bitI", P("p1"), 0.0, LT)
-                ts(("thb", 0, 1), ("thI", 0, 1), -1.0, MUL, 0.5, ADD)
-                ts(("fH", 0, 1), ("pI", 0, 1), 10, AND)
-                ts(("dcol", 0, 1), ("fH", 0, 1), 2.0, EQ)
-                ts(("scol", 0, 1), ("dcol", 0, 1), -2.0, MUL, 1.0, ADD)
+        scatter(0, 800)
+        cp("side16", P("p1"))
+        ts(("thb", 0, 1), ("thI", 0, 1), -1.0, MUL, 0.5, ADD)
+        ts("bitI", P("p1"), 0.0, LT)
+        scatter(800, NW)
+        extI("p2", "X", "itm")
         x_rows(0, L("LH", O_PAR), L("LL", O_PAR))
         gather("act", "SG", ("W", 0, NW), "side16", 0, H)
 
     def after_verdict0():
-        make_z("js", "jn", "sb1", "i2bn", "sg1", "a1")
-        for t in range(2):
-            act(("KW%d" % t, NI, NI + 1), ("dcol", 0, 1), AF.Copy)
+        make_z("pd", "kp")
+        asel("npre", T.npre[:], "n2560", T.n2560[:], [[-1, NC]], GE_, 0.0, UA // 16 - 1, 0)
+        make_z("r", "drop", "js", "jzp")
         gather("act", "SG", ("W", 0, NW), "side16", H, NW)
         act("sA0", P("p1"), AF.Relu)
         act("nbI", "bitI", AF.Identity, 1.0, -1.0)
-        ms(("Ub", NW, NW + 16), 0.0)
         mm(P("p3"), "M2", "bitI", True, False)
         mm(P("p6"), "NId", L("LH", O_SIDE), True, False)
         mm(P("p6"), "NId", L("LL", O_SIDE), False, False)
         extI("p0", "SG", "sg0", 0, H, False, False)
-        extI("p2", "X", "itm")
+        extB("p6", "SG", "side", 0, 8, False, False)
         extI("p0", "SG", "sg0", H, NW, False, True)
-        extI("p3", "SW", "a0", 0, NW, False, True)
+        extI("p3", "GE", "a0", 0, NW, False, True)
         cp("ip16", P("p2"))
-        gather("act", "Ua", ("Ua", 0, NW), "par16", 0, UA // 2, shift=NW)
-        act("kaT", P("p0"), AF.Identity, -1024.0)
-        gather("act", "Ua", ("Ua", 0, NW), "par16", UA // 2, UA, shift=NW)
+        gather("act", "Ua", ("Ua", 0, NW), "par16", 0, 480, shift=NW)
+        act("kaT", P("p0"), AF.Identity, -4096.0)
+        gather("act", "Ua", ("Ua", 0, NW), "par16", 480, UA, shift=NW)
         add_own(0, "Ua")
-        extI("p7", "SW", "n")
-        extB("p6", "SG", "side", 0, 16, False, True)
-        tt("t2", P("p3"), "kaT", MIN)
-        ts("ka16", "t2", 3072.0, ADD, 1024.0, MIN)
+        iota(("ZZ", ZL * ZW, len(ZS) * ZW), [[0, (len(ZS) - ZL) * ZW]])
+        make_z("jzm", "jn", "sb1", "i2bn", "sg1", "a1")
+        extI("p7", "GE", "n")
+        extB("p6", "SG", "side", 8, 16, False, True)
 
     def late_lists0():
         tt("bpI", P("p7"), "bitI", MUL)
         tt("t3", P("p7"), "nI", SUB)
         mm(P("p4"), "IDf", "sA0", True, False)
         mm(P("p4"), "IDf", "bpI", False, True)
+        act("DH", "t3", AF.Copy)
 
     def late_lists1():
-        act("DH", "t3", AF.Copy)
-        act("SH", P("p6"), AF.Copy)
         cp("pt16", P("p4"))
         tt("DL", "t3", "DH", SUB)
 
-    def w_half(bank, z, h):
-        return lambda: extI(bank, "W", z, HALF[h][0], HALF[h][1])
+    def w_half(bank, win, z, h):
+        return lambda: extI(bank, win, z, HALF[h][0], HALF[h][1])
 
-    def lists1a():
-        cp("par16", P("p2"))
-        tt("t1", "predI", "bpI", SUB)
-
-    def lists1b():
-        tt("t2", "t1", "sA1", ADD)
-        cp("pt16", "t2")
-
-    def par_digits():
-        cp("pJ", "pB")
-        ts("pK", "pJ", 0xFF0, AND)
-        cp("qH", "pK")
-        tt("qL", "pJ", "pK", SUB)
+    spare1 = [lambda: cp("pJ", "pB"),
+              lambda: ts("pK", "pJ", 0xFF0, AND),
+              lambda: cp("qH", "pK"),
+              lambda: tt("qL", "pJ", "pK", SUB),
+              lambda: cp("par16", P("p2")),
+              lambda: tt("t1", "predI", "bpI", SUB)]
 
     def par_rows():
         row("sp", "pr1", "W", R_PAR, "qH")
         row("sp", "pr1", "W", R_PAR + 1, "qL")
 
     def before_verdict1():
-        gather("act", "C", ("W", 0, NW), "pt16", 0, NW)
+        act("sA1", P("p3"), AF.Relu, -4096.0)
+        gather("act", "X", ("W", 0, NW), "par16", 0, NW)
+        mm(P("p1"), "IDf", "t1", True, False)
+        mm(P("p1"), "IDf", "sA1", False, True)
         extI("p2", "W", "i2bn", 0, NW, True, False)
-        gather("dve", "X", ("W", 0, NW), "par16", 0, NW)
         x_rows(1, "pH", "pL")
-        gather("dve", "Uc", ("Uc", 0, NW), "par16", 0, UA, shift=NW)
+        gather("dve", "Uc", ("Uc", 0, NW), "par16", 960, UA, shift=NW)
+        cp("pt16", P("p1"))
+        gather("dve", "Uc", ("Uc", 0, NW), "par16", 640, 960, shift=NW)
+        gather("dve", "C", ("W", 0, NW), "pt16", 0, H)
+        gather("dve", "C", ("W", 0, NW), "pt16", H, NW)
 
     def after_verdict1():
+        gather("act", "Uc", ("Uc", 0, NW), "par16", 0, 640, shift=NW)
         add_own(1, "Uc")
-        extI("p1", "C", "side")
-        extI("p2", "C", "sg1", 0, NW, False, True)
-        extI("p7", "X", "itm")
         mm(P("p3"), "M2", "nbI", True, False)
-        extI("p3", "C", "a1", 0, NW, False, False)
-        ts("z0", P("p1"), 0.0, EQ, 1024.0, MUL)
-        mm(P("p3"), "IDb", "z0", False, True)
-        cp("ip16", P("p7"))
-        act("kaT", P("p2"))
+        for h, (a, b) in enumerate(HALF):
+            extI("p2", "C", "sg1", a, b, False, h == 1)
+            extI("p3", "C", "a1", a, b, False, h == 1)
+        extI("p7", "X", "itm")
+        act("kaT", P("p2"), AF.Identity, 1024.0 - 2 * BIG)
         tt("t2", P("p3"), "kaT", MIN)
-        ts("ka16", "t2", 3072.0, ADD, 1024.0, MIN)
+        ts("ka16", "t2", 2048.0 + 2 * BIG, ADD, 1024.0, MIN)
+        cp("ip16", P("p7"))
 
     def splice_merge(t, U, U1, U2):
         kw = ("KW%d" % t, 0, NI + 1)
         arr = [verdicts_in(t)]
-        bank = ["p0", "p1"]
+        bank = ["p0", "p1", "p3"]
 
-        def cvt(lst, h):
-            cp((lst, 80 * h, 80 * (h + 1)), P(bank[h], 80))
-        mm(P("p5"), "IDf", "npre", True, False)
-        mm(P("p2"), "IDf", "sA%d" % t, True, False)
-        for h in range(2):
-            a, b = HALF[h]
+        def cvt(lst, q):
+            a, b = PART[q]
+            cp((lst, a // 16, b // 16), P(bank[q], (b - a) // 16))
+
+        def drop(h):
+            extI("p2", "KA", "drop", HALF[h][0], HALF[h][1], False, False)
+
+        def verdicts(a, b):
             gather("dve", "A", kw, "ip16", a, b, "X", MUL, ext=arr)
-            extI(bank[h], "A", "r", a, b, o=0)
-            extI("p5", "A", "kp", a, min(b, UA), False, False)
-            if h == 0 and t == 0:
-                late_lists0()
-        gather("act", "KA", kw, "ka16", 0, NW, ext=arr)
+        mm(P("p5"), "IDf", "npre", True, False)
         if t == 0:
-            late_lists1()
-        cvt("j1", 0)
+            verdicts(0, FIRST)
+            tt("t2", P("p3"), "kaT", MIN)
+            verdicts(FIRST, FIRST + 160)
+            ts("ka16", "t2", 6144.0, ADD, 1024.0, MIN)
+        gather("act", "KA", kw, "ka16", 0, H, ext=arr)
+        for q, (a, b) in enumerate(PART):
+            if q == 2:
+                verdicts(a, a + 384)
+                cvt("j1", 0)
+                if t == 0:
+                    late_lists1()
+            verdicts(FIRST + 160 if q == t == 0 else a + 384 * (q == 2), b)
+            extI(bank[q], "A", "r", a, b, o=0)
+            if q == 0:
+                if t == 0:
+                    late_lists0()
+                gather("act", "KA", kw, "ka16", H, NW)
+                mm(P("p2"), "IDf", "sA%d" % t, True, False)
+            if q == 1:
+                extI("p5", "A", "kp", 0, UA, False, False)
         chain = [("B", "A", "j1", "j2"), ("A", "B", "j2", "j4l"), ("B", "A", "j4l", None)]
         for lv, (o, win, lst, nxt) in enumerate(chain):
-            for h in range(2):
-                a, b = HALF[h]
-                gather("act", o, win, lst, a, a + SPLIT)
-                gather("dve", o, win, lst, a + SPLIT, b)
-                if h == 0:
-                    cvt(lst, 1)
-                extI(bank[h] if nxt else "p2", o, "r" if nxt else "jzm", a, b, nxt is not None, nxt is not None,
-                     0 if nxt else None)
-                if lv == 0 and h == 0:
+            for q, (a, b) in enumerate(PART):
+                m = a + SPLIT[q]
+                gather("act", o, win, lst, a, m)
+                if q != 1:
+                    gather("dve", o, win, lst, m, m + 192)
+                    m += 192
+                    if q == 0:
+                        cvt(lst, 1)
+                    elif nxt:
+                        cvt(nxt, 0)
+                gather("dve", o, win, lst, m, b)
+                if q == 0:
+                    cvt(lst, 2)
+                if q == 1 and lv == 1:
+                    cp("pe16", P("p5"))
+                if q == 0 and lv == 2:
+                    drop(1)
+                if nxt:
+                    extI(bank[q], o, "r", a, b, o=0)
+                else:
+                    extI("p5", o, "js", a, b)
+                if lv == 0 and q == 0:
                     extI("p5", "A", "pd", UA, NW, False, True)
-                if h == 0 and lv > 0:
-                    extI("p2", "KA", "drop", HALF[lv - 1][0], HALF[lv - 1][1], False, False)
-            if nxt:
-                cvt(nxt, 0)
-            if lv == 1:
-                cp("pe16", P("p5"))
+                if q == 0 and lv == 1:
+                    drop(0)
         row("sp", "rp%d" % t, "A", 0, "nIH")
         row("sp", "rp%d" % t, "A", 1, "nIL")
-        for h in range(2):
-            a, b = HALF[h]
-            gather("act", "C", "B", "pt16", a, a + PSPLIT)
-            gather("dve", "C", "B", "pt16", a + PSPLIT, b)
+        for h, (a, m, b) in enumerate(((0, 768, 1600), (1600, 2080, NW))):
+            gather("act", "C", "B", "pt16", a, m)
+            gather("dve", "C", "B", "pt16", m, b)
             extI("p2", "C", "jzp", a, b, False, h == 1)
-        extI("p1", "B", "js")
+            if h == 0:
+                act("t1", P("p5"), AF.Identity, 0.0, -4096.0)
+                mm(P("p2"), "IDf", "t1", False, False)
         def spliced(j):
             a, b = PIECE[j]
             if a < UA:
@@ -622,59 +713,69 @@ def rank_program(g, core, T, topo):
             else:
                 gather("dve", U1, (U, 0, NW), "pe16", a, b, U, ADD, shift1=NW)
             return lambda: dma("sp", "ud%d_%d" % (t, j), T.Ud[:, a:b], T[U1][:, a:b], [(U1, a, b)], [("Ud", a, b)])
-        spliced(0)()
-        spliced(1)
+        spliced(2)
+        spliced(0)
+        cp("p816", P("p5"))
+        cp(("Ud",) + PIECE[2], (U1,) + PIECE[2])
         ts("mI", P("p2"), 0.0, EQ)
+        ts("se16", P("p2"), float(NW), MIN, 0.0, MAX)
         tt("dH", "mI", "DH", MUL)
         row("sp", "rp%d" % t, "A", 2, "dH")
         tt("dL", "mI", "DL", MUL)
         row("sp", "rp%d" % t, "A", 3, "dL")
-        ts("se16", P("p2"), float(NW), MIN, 0.0, MAX)
-        spliced(2)()
+        if t == 0:
+            act("SH", P("p6"), AF.Copy)
+        copy1 = spliced(1)
         spliced(3)()
-        act(("Ud",) + PIECE[1], (U1,) + PIECE[1], AF.Copy)
-        cp("p816", P("p1"))
+        copy1()
+        act(("Ud",) + PIECE[0], (U1,) + PIECE[0], AF.Copy)
         if t == 0:
             tt("SL", P("p6"), "SH", SUB)
             act("predI", P("p7"))
             extB("p3", "KA", "drop", 0, 16, True, False)
             extB("p3", "B", "jzm", 0, 16, False, False)
             extB("p3", "C", "jzp", 0, 16, False, True)
-        for j, (a, b) in enumerate(TAIL):
-            gather("act", "SG", "A", "p816", a, b)
-            gather("dve", U2, (U1, 0, NW + 1), "se16", PIECE[j][0], PIECE[j][1], "Ud", ADD)
-            if t == 0 and j == 3:
-                ge4(U2, 0, 960, True)
-            extB("p4", "SG", "jn", a // NC, b // NC, a == 0, b == NW)
-            if t == 1:
-                a, b = PIECE[j]
+        def finish(j):
+            a, b = PIECE[LAST[j]]
+            if t == 0:
+                ge4(U2, a, b, j == 0, last=j == 3)
+            else:
                 ts(("Y", a, b), (U2, a, b), 15.0, MIN)
                 dma("sp", "yc%d" % j, T.yc[:, a:b], T.Y[:, a:b], [("Y", a, b)], [])
+        for j, (a, b) in enumerate(TAIL):
+            gather("act", "SG", "A", "p816", a, b)
+            gather("dve", U2, (U1, 0, NW + 1), "se16", PIECE[LAST[j]][0], PIECE[LAST[j]][1], "Ud", ADD)
+            extB("p4", "SG", "jn", a // NC, b // NC, a == 0, b == NW)
+            if t == 0 and j == 2:
+                ts("mB", P("p3"), 0.0, EQ)
+            if j and not (t == 0 and j == 3):
+                finish(j - 1)
+            if t == 0 and j == 2:
+                for f, o, d in ((R_DS, "sH", "SH"), (R_DS + 1, "sL", "SL")):
+                    tt(o, "mB", d, MUL)
+                    row("sp", "sd1", "W", f, o)
+                add_up("p4", [("NId", x) for x in (L("LH", O_SIDE), L("LL", O_SIDE), "sH", "sL")], False, False)
+                finish(2)
+        finish(3)
         if t == 0:
-            ge4(U2, 960, 1920, False)
-            ge4(U2, 1920, NW, False)
-            act("pH", P("p4"), AF.Copy)
-            act(("Y", 9 * NC, NW), (U2, 9 * NC, NW), AF.Relu, 15.0, -1.0)
-            ts("mB", P("p3"), 0.0, EQ)
-            for f, o, d in ((R_DS, "sH", "SH"), (R_DS + 1, "sL", "SL")):
-                tt(o, "mB", d, MUL)
-                row("sp", "sd1", "W", f, o)
-            tt("pL", P("p4"), "pH", SUB)
-            act("pB", P("p4"))
+            act(("Y", UA, NW), (U2, UA, NW), AF.Relu, 15.0, -1.0)
+            act("eH", P("p4"), AF.Copy)
+            act(("Y", 9 * NC, UA), (U2, 9 * NC, UA), AF.Relu, 15.0, -1.0)
         else:
-            act("ypB", P("p4"))
-            dma("act", "yp0", T.yp[:], T.ypB[:], ["ypB"], [])
+            act("pB", P("p4"))
+            dma("act", "yp0", T.yp[:], T.pB[:], ["pB"], [])
 
     prep(0, "Ua")
-    walks(0, [lambda: extI("p3", "W", "par"), w_half("p2", "side", 0), w_half("p2", "side", 1), nop],
-          [consts0, consts1, consts2], [aconsts0, aconsts1, nop], late_rows, nop)
+    walks(0, [w_half("p3", "W", "par", 0), w_half("p3", "W", "par", 1), lambda: extI("p2", "W", "side"), nop],
+          [aconsts0, selectors], spare0, late_rows)
     before_verdict0()
     verdict(0)
     after_verdict0()
     splice_merge(0, "Ua", "Ub", "Uc")
     prep(1, "Uc")
-    walks(1, [lambda: extI("p2", "SG", "jn"), w_half("p3", "sb1", 0), w_half("p3", "sb1", 1), nop], [par_digits, lists1a, nop],
-          [nop, nop, lambda: act("sA1", P("p3"), AF.Relu, -4096.0)], par_rows, lists1b)
+    extI("p2", "SG", "jn", 0, H)
+    walks(1, [w_half("p2", "SG", "jn", 1), w_half("p3", "W", "sb1", 0), w_half("p3", "W", "sb1", 1), nop], [nop, nop],
+          spare1, par_rows)
     before_verdict1()
     verdict(1)
     after_verdict1()

from concourse.bass import DstId, RemoteDMATransfer
from concourse.mybir import AluOpType, ActivationFunctionType

NW, NI, NC = 2560, 1024, 160
H = NW // 2
R_N, R_PAR, R_PU, R_SIDE, R_ITM, R_DS, R_ONE, R_UP, R_BIT = 0, 2, 4, 6, 8, 10, 12, 13, 14
R_NZ = R_ONE
BIG = 2.0 ** 22


def pair(r, w=1.0):
    return {r: w, r + 1: w}


def sigma(w):
    return {0: w / 16, 1: 160 * w, 2: w / 16, 3: 160 * w}


ZS = [
    ("all", None, None),
    ("n", None, pair(R_N)),
    ("side", None, {R_SIDE: 1.0, R_SIDE + 1: 1.0, R_DS: 1.0, R_DS + 1: 1.0}),
    ("x", "side", {R_UP: 4096.0}),
    ("lin", "side", {R_PU: 1.0, R_PU + 1: 1.0, R_UP: 2560.0}),
    ("par", None, pair(R_PAR)),
    ("sb0", "side", {R_BIT: -4096.0}),
    ("itm", None, pair(R_ITM)),
    ("i2b", "itm", {R_BIT: 2048.0}),
    ("sg0", None, {R_BIT: -1024.0, R_NZ: -1024.0}),
    ("a0", "itm", {R_BIT: 1024.0, R_ONE: -4096.0}),
    ("pd", None, pair(6)),
    ("r", "pd", pair(4)),
    ("kp", None, {R_ONE: -2560.0}),
    ("drop", None, {2: 2.0 ** 24}),
    ("jzm", None, sigma(-4096.0)),
    ("jzp", None, sigma(4096.0)),
    ("js", None, sigma(1.0)),
    ("jn", "n", pair(2)),
    ("sb1", "side", {R_BIT: 4096.0}),
    ("i2bn", "itm", {R_BIT: -2048.0}),
    ("sg1", None, {R_BIT: 1024.0, R_NZ: -1024.0}),
    ("a1", "itm", {R_BIT: -BIG, R_NZ: -BIG, R_DS: -1024.0, R_DS + 1: -1024.0}),
]
ZI = {z[0]: k for k, z in enumerate(ZS)}
ZE = 6
ZM = 11
ZL = 19
ZW = 144
UA = 1600

SCRATCH = {}
for _n in ("A", "B", "C", "KA", "Y", "UM", "SG", "X", "Ud"):
    SCRATCH[_n] = ("sbuf", [128, NW], "bfloat16")
SCRATCH["Ub"] = ("sbuf", [128, NW + 16], "bfloat16")
for _n in ("W", "GE", "Ua", "Uc"):
    SCRATCH[_n] = ("sbuf", [128, 2 * NW], "bfloat16")
for _n in ("F0", "F1", "G0", "G1", "G2", "S", "ACC0", "ACC1", "LAND0", "LAND1"):
    SCRATCH[_n] = ("sbuf", [128, NI], "bfloat16")
for _n in ("KW0", "KW1"):
    SCRATCH[_n] = ("sbuf", [128, NI + 16], "bfloat16")
SCRATCH["ZZ"] = ("sbuf", [128, len(ZS) * ZW], "bfloat16")
SCRATCH["BZ"] = ("sbuf", [128, 16 * 128], "bfloat16")
for _n in ("IDb", "NId", "M2", "BO", "s1", "c15"):
    SCRATCH[_n] = ("sbuf", [128, 128], "bfloat16")
for _n in ("IDf", "tot"):
    SCRATCH[_n] = ("sbuf", [128, 128], "float32")
O_HEAD, O_PAR, O_SIDE, O_ITM, O_BIT, O_END = 0, 64, 224, 384, 544, 704
for _n in ("LI", "HI"):
    SCRATCH[_n] = ("sbuf", [128, O_END], "int32")
for _n in ("LH", "LL"):
    SCRATCH[_n] = ("sbuf", [128, O_END], "bfloat16")
for _n in ("nI", "n2560", "npre", "predI", "sA0", "sA1", "t1", "t2", "t3", "kaT", "bpI", "pB"):
    SCRATCH[_n] = ("sbuf", [128, NC], "float32")
for _n in ("pJ", "pK"):
    SCRATCH[_n] = ("sbuf", [128, NC], "int32")
for _n in ("upB", "puH", "puL", "eH", "eL", "euH", "euL", "dH", "dL", "sH", "sL", "pH", "pL", "qH", "qL", "DH", "DL", "mB", "mI", "SH", "SL", "bitI",
           "nbI", "nBH", "nBL", "nIH", "nIL", "cB", "nzB", "oneB"):
    SCRATCH[_n] = ("sbuf", [128, NC], "bfloat16")
for _n in ("par16", "side16", "ip16", "sc16", "ka16", "pt16", "j1", "j2", "j4l", "pe16", "p816", "se16"):
    SCRATCH[_n] = ("sbuf", [128, NC], "uint16")
for _n in ("hd16", "ix1", "ix2", "w1", "w2", "w3"):
    SCRATCH[_n] = ("sbuf", [128, 64], "uint16")
for _n in ("k0", "k1", "wa", "wb", "wu"):
    SCRATCH[_n] = ("sbuf", [128, 64], "float32")
for _n in ("thI", "pI", "fI", "fH"):
    SCRATCH[_n] = ("sbuf", [128, 4], "int32")
for _n in ("thb", "fF", "f160", "dcol", "scol"):
    SCRATCH[_n] = ("sbuf", [128, 4], "float32")
SCRATCH["OH"] = ("sbuf", [128, 16], "float32")
SCRATCH["z8"] = ("sbuf", [128, 8], "bfloat16")
for _k in range(8):
    SCRATCH["p%d" % _k] = ("psum", [128, 512], "float32")

ENG = ["pe", "dve", "act", "pool"]
DMAG = ["ldh", "ldp", "ldi", "ldu0", "ldu1", "ldu2", "ldu3", "ldth", "hd0", "late", "swz", "fw0", "fx0", "fw1", "fx1", "rp0", "rp1",
        "sd1", "pr1", "vv0", "vv1", "xr0", "xr1", "ya0", "ya1", "yc0", "yc1", "yc2", "yc3", "yp0", "uu0", "uu1"] + \
    ["ud%d_%d" % (_t, _j) for _t in range(2) for _j in (1, 3)]
SEMAPHORES = ["e_" + _e for _e in ENG] + ["d_" + _d for _d in DMAG] + ["sent"] + \
    ["rs%d_%d" % (_t, _m) for _t in range(2) for _m in range(4)] + ["ag0", "ag1"]

ADD, SUB, MUL, MAX, MIN = AluOpType.add, AluOpType.subtract, AluOpType.mult, AluOpType.max, AluOpType.min
GE_, LT, EQ, NE = AluOpType.is_ge, AluOpType.is_lt, AluOpType.is_equal, AluOpType.not_equal
AND = AluOpType.bitwise_and
AF = ActivationFunctionType
FIRST = 448
PART = [(0, 896), (896, 1792), (1792, NW)]
SPLIT = (512, 480, 416)
CUT = ((704, 768, 640), (640, 704, 576))
FILL = ((2, 2, 1), (1, 1, 0))
PAIRS = (2, 3, 1, 0)
TAIL = [(640 * _j, 640 * (_j + 1)) for _j in range(4)]
HALF = [(0, H), (H, NW)]
LOAD = [(0, 800), (800, 1600), (1600, 2240), (2240, NW)]
PIECE = [(0, 800), (800, UA), (UA, 2080), (2080, NW)]
LAST = (2, 0, 3, 1)


def rank_program(g, core, T, topo):
    rank = T.rank_of(core)
    if rank is None:
        return
    N = len(T.cores)
    Q = {"pe": g.tensor, "dve": g.vector, "act": g.scalar, "pool": g, "sp": g.sync}
    ops = []
    sent = [0]

    def reg(x):
        if isinstance(x, str):
            return (x, 0, 1 << 20, None)
        return (x[0], x[1], x[2], x[3] if len(x) > 3 else None)

    def op(eng, fn, r=(), w=(), grp=None, ext=(), inc=True):
        ops.append({"e": eng, "fn": fn, "r": [reg(x) for x in r], "w": [reg(x) for x in w], "grp": grp, "ext": list(ext),
                    "inc": inc})

    def ap(x):
        x = reg(x)
        if x[2] == 1 << 20:
            return T[x[0]][:]
        return T[x[0]][:, x[1]:x[2]]

    def col(s):
        if isinstance(s, str):
            return T[s][:, 0:1], [s]
        if isinstance(s, tuple):
            return ap(s), [s]
        return s, []

    def ts(o, i, s1, op0, s2=None, op1=None):
        a1, rd = col(s1)
        if op1 is None:
            op("dve", lambda: g.vector.tensor_scalar(ap(o), ap(i), a1, None, op0), [i] + rd, [o])
        else:
            op("dve", lambda: g.vector.tensor_scalar(ap(o), ap(i), a1, s2, op0, op1), [i] + rd, [o])

    def tt(o, a, b, alu):
        op("dve", lambda: g.vector.tensor_tensor(ap(o), ap(a), ap(b), alu), [a, b], [o])

    def cp(o, i):
        op("dve", lambda: g.vector.tensor_copy(ap(o), ap(i)), [i], [o])

    def ms(o, v):
        op("dve", lambda: g.vector.memset(ap(o), v), [], [o])

    def act(o, i, func=AF.Identity, bias=0.0, scale=1.0):
        b, rb = col(bias)
        s, rs = col(scale)
        op("act", lambda: g.scalar.activation(ap(o), ap(i), func, bias=b, scale=s), [i] + rb + rs, [o])

    def gather(eng, o, win, lst, a, b, in1=None, alu=None, ext=(), shift=0, shift1=0):
        l = (lst, a // 16, b // 16)
        out = (o, shift + a, shift + b)
        rd = [win, l] + ([(in1, shift1 + a, shift1 + b)] if in1 else [])
        if eng == "act":
            fn = lambda: g.scalar.activation(ap(out), ap(win).indirect(ap(l)), AF.Copy)
        elif in1:
            fn = lambda: g.vector.tensor_tensor(ap(out), ap(win).indirect(ap(l)), ap(rd[2]), alu)
        else:
            fn = lambda: g.vector.tensor_copy(ap(out), ap(win).indirect(ap(l)))
        op(eng, fn, rd, [out], ext=ext)

    def sel(z, i):
        z0 = ZI[z] * ZW
        return T.ZZ[:, z0 + 16 - i:z0 + ZW - i]

    def zreg(z):
        return ("ZZ", ZI[z] * ZW, (ZI[z] + 1) * ZW)

    def extI(bank, src, z, a=0, b=NW, start=True, stop=True, o=None):
        o0 = a // 16 if o is None else o

        def fn():
            for i in range(16):
                ins = g.tensor.matmul(T[bank][:, o0:o0 + (b - a) // 16], sel(z, i), T[src][:, a + i:b:16],
                                      start and i == 0, stop and i == 15)
            return ins
        op("pe", fn, [(src, a, b), zreg(z)], [bank])

    def extB(bank, src, z, i0=0, i1=16, start=True, stop=True):
        def fn():
            for i in range(i0, i1):
                ins = g.tensor.matmul(T[bank][:, 0:NC], sel(z, i), T[src][:, NC * i:NC * (i + 1)],
                                      start and i == i0, stop and i == i1 - 1)
            return ins
        op("pe", fn, [(src, NC * i0, NC * i1), zreg(z)], [bank])

    def spread(bank, src, i0, i1, lhs=None, win=None):
        if lhs:
            mm(P(bank, NC * (i1 - i0)), lhs, (win, NC * i0, NC * i1), True, False)

        def fn():
            for i in range(i0, i1):
                ins = g.tensor.matmul(T[bank][:, NC * (i - i0):NC * (i - i0 + 1)], T.BZ[:, 128 * i:128 * (i + 1)], T[src][:],
                                      not win, not win or i == i1 - 1)
            return ins
        op("pe", fn, [src, ("BZ", 128 * i0, 128 * i1)], [bank])

    def mm(o, lhs, rhs, start, stop, ext=()):
        op("pe", lambda: g.tensor.matmul(ap(o), T[lhs][:], ap(rhs), start, stop), [lhs, rhs], [o], ext=ext)

    def add_up(bank, terms, start=True, stop=True):
        for j, (lhs, x) in enumerate(terms):
            mm(P(bank), lhs, x, start and j == 0, stop and j == len(terms) - 1)

    def dma(q, grp, out, in_, r, w, ext=()):
        op(q, lambda: Q[q].dma_start(out, in_), r, w, grp=grp, ext=ext)

    def row(q, grp, win, f, src, c0=0, n=NW, ext=()):
        dma(q, grp, T[win][f::16, c0:c0 + n], ap(src), [src], [(win, c0, c0 + n, f)], ext)

    def P(bank, n=NC, o=0):
        return (bank, o, o + n)

    def L(buf, o, n=NC):
        return (buf, o, o + n)

    def digits(o, n):
        ts(L("HI", o, n), L("LI", o, n), 0xFF0, AND)
        cp(L("LH", o, n), L("HI", o, n))
        tt(L("LL", o, n), L("LI", o, n), L("HI", o, n), SUB)

    def dst(r):
        rid, pid = topo.addr(T.cores[r], core)
        return DstId(rid=rid, pnc=pid)

    def engs(r, part, parts):
        e = topo.engines(core, T.cores[r])
        k = len(e) // parts
        return e[part * k:(part + 1) * k]

    def bits(e):
        return sum(1 << x for x in e)

    def iota(o, pat, cm=0, small=True):
        if small:
            op("pool", lambda: g.iota(ap(o), pat, 0, cm, allow_small_or_imprecise_dtypes=True), [], [o])
        else:
            op("pool", lambda: g.iota(ap(o), pat, 0, cm), [], [o])

    def asel(o, oap, i, iap, pat, cmp, fill, base, cm):
        op("pool", lambda: g.affine_select(oap, iap, pat, cmp, fill, base, cm), [i], [o])

    def make_z(*names):
        view = lambda z: T.ZZ[:, ZI[z] * ZW + 16:(ZI[z] + 1) * ZW:16]
        for j in range(4):
            for name in names:
                _, base, wts = ZS[ZI[name]]
                if j < len(wts):
                    f, src = sorted(wts)[j], name if j else base or name
                    asel(zreg(name), view(name), zreg(src), view(src), [[-16, 8]], NE, wts[f], -f, 1)

    def zero(o, i):
        act(o, i, AF.Identity, 0.0, 0.0)

    def load(q, grp, name, o, n):
        dma(q, grp, T.LI[:, o:o + n], T[name][:], [], [L("LI", o, n)])

    load("sp", "ldh", "heads", O_HEAD, 64)
    load("act", "ldp", "par", O_PAR, NC)
    load("sp", "ldp", "side", O_SIDE, NC)
    for j, (a, b) in enumerate(LOAD):
        dma("sp", "ldu%d" % j, T.Ua[:, a:b], T.cnt[:, a:b], [], [("Ua", a, b)])
    iota(("pI", 0, 1), [[0, 1]], 1, False)
    iota("OH", [[1, 16]])
    ms("c15", 15.0)
    ms("IDb", 1.0)
    ts(("fH", 0, 1), ("pI", 0, 1), 10, AND)
    ms(("ZZ", 0, ZE * ZW), 0.0)
    ts(("dcol", 0, 1), ("fH", 0, 1), 2.0, EQ)
    ts(("fI", 0, 1), ("pI", 0, 1), 15, AND)
    ms(("W", NW, NW + H), 0.0)
    ts(("scol", 1, 2), ("dcol", 0, 1), 240.0, MUL, -120.0, ADD)
    cp(("fF", 0, 1), ("fI", 0, 1))
    ms(("W", 0, NW), 0.0)
    ts("OH", "OH", "fF", EQ)
    asel("BO", T.BO[:], "c15", T.c15[:], [[-16, 8], [0, 16]], GE_, 0.0, 0, 1)
    asel("z8", T.z8[:], "IDb", T.IDb[:, 0:8], [[-16, 8]], GE_, 0.0, 0, 1)
    asel("BO", T.BO[:], "BO", T.BO[:], [[16, 8], [0, 16]], GE_, 0.0, 15, -1)
    asel(zreg("all"), T.ZZ[:, 16:ZW:16], "z8", T.z8[:], [[16, 8]], GE_, 0.0, 15, -1)
    asel("IDb", T.IDb[:], "IDb", T.IDb[:], [[-1, 128]], EQ, 0.0, 0, 1)
    act(("W", NW + H, 2 * NW), ("W", NW, NW + H), AF.Copy)
    act("NId", "IDb", AF.Identity, 0.0, -1.0)

    def spreader(i):
        act(("BZ", 128 * i, 128 * (i + 1)), "BO", AF.Identity, 0.0, ("OH", i, i + 1))
    for i in range(9):
        if i == 6:
            make_z("par", "side")
        z = ("BZ", 128 * i, 128 * (i + 1))
        asel(z, ap(z), "c15", T.c15[:], [[-16, 8], [0, 16]], EQ, 0.0, -i, 1)
    make_z("lin", "x")
    iota("nI", [[16, NC]])
    iota("cB", [[1, NC]])
    iota("nBL", [[0, 10], [1, 16]])
    iota("nBH", [[16, 10], [0, 16]])
    iota("nIH", [[16, NC]])
    op("pool", lambda: g.dma_start(T.thI[:, 0:1], T.th[:], allow_slow_non_contiguous=True), [], [("thI", 0, 1)], grp="ldth")
    parts = ((O_HEAD, 64), (O_PAR, 2 * NC))
    for o, n in parts:
        ts(L("HI", o, n), L("LI", o, n), 0xFF0, AND)
    for o, n in parts:
        cp(L("LH", o, n), L("HI", o, n))
        tt(L("LL", o, n), L("LI", o, n), L("HI", o, n), SUB)
    row("sp", "hd0", "W", R_PAR, L("LH", O_HEAD, 64), NW, NI)
    row("sp", "hd0", "W", R_PAR + 1, L("LL", O_HEAD, 64), NW, NI)
    for f, o in ((R_SIDE, O_SIDE), (R_PAR, O_PAR)):
        row("sp", "fw0", "W", f, L("LH", o))
        row("sp", "fw0", "W", f + 1, L("LL", o))

    def ge4(U, a, b, first, eng="dve", last=False):
        if eng == "dve":
            ts(("GE", a, b), (U, a, b), 4.0, GE_, 0.5, SUB)
        else:
            act(("GE", a, b), (U, a, b), AF.Sign, -3.5)
        extB("p0", "GE", "all", a // NC, b // NC, first, last)

    def nop():
        pass

    def prep(t, U):
        if t == 0:
            add_up("p4", (("IDb", L("LH", O_PAR)), ("IDb", L("LL", O_PAR)), ("NId", L("LH", O_SIDE)),
                          ("NId", L("LL", O_SIDE))))
            for j, (a, b) in enumerate(LOAD):
                ge4(U, a, b, j == 0, "act" if j == 0 else "dve", j == 3)
                if j == 0:
                    for k in ("KW0", "KW1"):
                        act((k, NI, NI + 1), ("scol", 1, 2), AF.Sigmoid)
                    act("eH", P("p4"), AF.Copy)
                    for i in range(9, 16):
                        spreader(i)
                if j == 3:
                    tt("eL", P("p4"), "eH", SUB)
                    ts(("scol", 0, 1), ("dcol", 0, 1), -16.0, MUL, 8.0, ADD)
                    ms(("Ub", NW, NW + 16), 0.0)
                    ts(("f160", 0, 1), ("fF", 0, 1), 160.0, MUL)
            ph, pl = L("LH", O_PAR), L("LL", O_PAR)
        else:
            ph, pl = "pH", "pL"
        lhs, win = ("NId", "Y") if t else ("IDb", U)
        mm(P("p6", 3 * NC), lhs, (win, 13 * NC, 16 * NC), True, False)
        mm(P("p7", 2 * NC), lhs, (win, 11 * NC, 13 * NC), True, False)
        ts("upB", P("p0"), 0.5, GE_)
        row("sp", "fw%d" % t, "W", R_UP, "upB")
        if t == 0:
            ms("mI", 0.0)
        else:
            tt("eL", P("p4"), "eH", SUB)
        tt("euH", "eH", "upB", MUL)
        row("sp", "fw%d" % t, "W", R_PU, "euH")
        tt("euL", "eL", "upB", MUL)
        row("sp", "fw%d" % t, "W", R_PU + 1, "euL")
        if t == 0:
            extI("p1", "W", "par", NW, NW + NI, o=0)
            cp("hd16", P("p1", 64))

        def second_half():
            if t == 1:
                tt("pL", P("p3"), "pH", SUB)
                act("pB", P("p3"))
            tt("puH", ph, "upB", MUL)
            tt("puL", pl, "upB", MUL)
            for f, s in ((R_UP, "upB"), (R_PU, "puH"), (R_PU + 1, "puL")):
                row("sp", "fx%d" % t, "W", f, s, NW)
        if t == 0:
            act("IDf", "IDb")
        for (i0, i1), (k0, k1), b, c in (((0, 3), (13, 16), "p5", "p6"), ((3, 6), (11, 13), "p4", "p7"),
                                         ((6, 9), (9, 11), "p5", "p6")):
            spread(b, "upB", i0, i1)
            tt(("UM", NC * i0, NC * i1), P(b, NC * (i1 - i0)), (U, NC * i0, NC * i1), MIN)
            spread(c, "upB", k0, k1, lhs if i0 == 6 else None, win)
            act(("UM", NC * k0, NC * k1), P(c, NC * (k1 - k0)), AF.Relu, 0.0 if t else -15.0)
            if i0 == 0 and t == 1:
                add_up("p3", [("IDb", x) for x in (L("LH", O_SIDE), L("LL", O_SIDE), "sH", "sL", "eH", "eL")])
                act("pH", P("p3"), AF.Copy)
            if i0 == 3 * t:
                second_half()
        if t == 0:
            load("sp", "ldi", "itm", O_ITM, NC)
            load("sp", "ldi", "bit", O_BIT, NC)
            for f in (R_N, R_N + 1, R_ONE):
                row("sp", "swz", "GE", f, "mI")

    def walks(t, pe_fill, act_fill, spare, after_fields):
        acc = "ACC%d" % t

        def fill(n=1):
            for _ in range(n):
                if spare:
                    spare.pop(0)()

        gather("act", "F0", ("W", 0, NW), "hd16", 0, 512)
        gather("dve", "F0", ("W", 0, NW), "hd16", 512, NI)
        pe_fill[0]()
        for s in range(3):
            F, w, p = "F%d" % (s % 2), "w%d" % s if s else "hd16", P("p1", 64)
            extI("p1", F, "lin", 0, NI)
            if s == 1:
                mm(P("p0", 64), "IDf", "k0", True, False)
            if s < 2:
                extI("p0", F, "x", 0, NI, s == 0, True)
            gather("act", "G%d" % s, "UM", w, 0, CUT[t][s])
            gather("dve", "G%d" % s, "UM", w, CUT[t][s], NI)
            for h in range(2):
                mm("p%d" % (6 + h), "IDb", ("G%d" % s, 512 * h, 512 * (h + 1)), s == 0, s == 2)
            pe_fill[s + 1]()
            fill(FILL[t][s])
            if s:
                tt("wa", p, "k%d" % (s - 1), MAX)
            else:
                cp("ix1", p)
            ts("wu", p, float(NW), GE_, float(NW), MUL)
            if s == 1:
                cp("ix2", "wa")
            if s != 1:
                fill()
            tt("wb", "wa" if s else p, "wu", SUB)
            if s < 2:
                F = "F%d" % (1 - s)
                act_fill[s]()
                gather("act", F, "W", "ix%d" % (s + 1), 0, 608)
                gather("dve", F, "W", "ix%d" % (s + 1), 608, NI)
                if s == 1:
                    after_fields()
            else:
                fill()
            cp("w%d" % (s + 1), "wb")
            if s < 2:
                ts("k%d" % s, P("p0", 64), -4096.0, ADD, 0.0, MAX)
                fill()

        def sums(m):
            c = rank // 2 ^ PAIRS[m]
            act(("S", 256 * c, 256 * (c + 1)), ("p%d" % (6 + c // 2), 256 * (c % 2), 256 * (c % 2 + 1)), AF.Copy)
            gather("dve", acc, "UM", "w3", 256 * c, 256 * (c + 1), "S", ADD)
            to = senders(m)

            def send():
                tr = [RemoteDMATransfer(dst_ids=[dst(r)], dma_engine_mask=bits(engs(r, j, len(to))),
                                        remote_sem=T.sem["rs%d_%d" % (t, m)], src=T[acc][:, 128 * r:128 * (r + 1)],
                                        dst=T["LAND%d" % t][:, 128 * rank:128 * (rank + 1)]) for j, r in enumerate(to)]
                return g.remote_dma_fused(tr, local_sem=T.sem.sent)
            sent[0] += sum(len(engs(r, j, len(to))) for j, r in enumerate(to))
            op("pool", send, [(acc, 256 * c, 256 * (c + 1))], [], inc=False)
        for m in range(4):
            sums(m)
            if m:
                fill()
        fill(len(spare))

    def senders(m):
        c = rank // 2 ^ PAIRS[m]
        return [r for r in (2 * c, 2 * c + 1) if r != rank]

    def sums_in(t, m):
        return ("rs%d_%d" % (t, m), sum(len(topo.engines(T.cores[r], core)) // len(senders(m)) for r in senders(m)))

    def verdicts_in(t):
        return ("ag%d" % t, sum(len(topo.engines(T.cores[r], core)) for r in range(N) if r != rank))

    def verdict(t):
        acc, land, kw = "ACC%d" % t, "LAND%d" % t, "KW%d" % t
        own = (128 * rank, 128 * (rank + 1))
        mm(P("p4", 128), "IDb", (acc,) + own, True, False)
        for m in range(4):
            for r in senders(m):
                mm(P("p4", 128), "IDb", (land, 128 * r, 128 * (r + 1)), False, m == 3, ext=[sums_in(t, m)])
        act("s1", P("p4", 128), AF.Sign, "thb")
        mm(P("p5", 128), "BO", "s1", True, True)
        act((kw,) + own, P("p5", 128), AF.Sigmoid, ("scol", 1, 2), ("scol", 0, 1))
        oth = [(rank + d) % N for d in range(1, N)]

        def send():
            a = T[kw][:, own[0]:own[1]]
            tr = RemoteDMATransfer(dst_ids=[dst(r) for r in oth], dma_engine_mask=bits(engs(oth[0], 0, 1)),
                                   remote_sem=T.sem["ag%d" % t], srcs=[a], dsts=[a for r in oth])
            return g.remote_dma_fused([tr], local_sem=T.sem.sent)
        sent[0] += len(engs(oth[0], 0, 1))
        op("pool", send, [(kw,) + own], [], inc=False)
        act("tot", P("p4", 128))
        dma("sp", "ya%d" % t, T.ya[:, 128 * t:128 * (t + 1)], T.tot[:], ["tot"], [], [verdicts_in(t)])

    def x_rows(t, ph, pl):
        for f, s in ((4, "nBH"), (5, "nBL"), (6, ph), (7, pl)):
            row("sp", "xr%d" % t, "X", f, s, ext=[sums_in(t, 3)])

    def add_own(t, U):
        op("pool", lambda: g.dma_start(T[U][:, NW:NW + UA], T[U][:, 0:UA], accum_op=ADD, max_dma_last_dim=4096),
           [(U, 0, UA), (U, NW, NW + UA)], [(U, NW, NW + UA)], grp="vv%d" % t, ext=[verdicts_in(t)])
        dma("sp", "uu%d" % t, T[U][:, NW + UA:2 * NW], T[U][:, UA:NW], [(U, UA, NW)], [(U, NW + UA, 2 * NW)], [verdicts_in(t)])

    itm = [L(x, O_ITM) for x in ("LI", "HI", "LH", "LL")]
    spare0 = [lambda: ts("nI", "nI", "fF", ADD),
              lambda: ts("nzB", "cB", "f160", ADD, 0.0, NE),
              lambda: ts(itm[1], itm[0], 0xFF0, AND),
              lambda: cp(L("LH", O_BIT), L("LI", O_BIT)),
              lambda: cp(itm[2], itm[1]),
              lambda: tt(itm[3], itm[0], itm[1], SUB),
              lambda: cp("par16", P("p3")),
              lambda: ts("t1", P("p2"), 0.0, EQ, 8192.0, MUL),
              lambda: tt("t2", "t1", "n2560", MIN),
              lambda: tt("t3", P("p2"), "t2", ADD),
              lambda: cp("sc16", "t3")]

    def scatter(a, b):
        l = ("sc16", a // 16, b // 16)
        op("dve", lambda: g.vector.tensor_copy(T.GE[:].indirect(ap(l)), T.W[:, a:b]), [l, ("W", a, b)], ["GE"])

    def aconsts0():
        act("nBH", "nBH", AF.Identity, "f160")
        act("n2560", "nI", AF.Identity, float(NW))

    def selectors():
        iota(("ZZ", ZE * ZW, ZM * ZW), [[0, (ZM - ZE) * ZW]])
        make_z("itm", "sb0", "n", "sg0")
        make_z("a0", "i2b")

    def aconsts1():
        act("nIL", "cB", AF.Identity, "fF", 0.0)
        act("M2", "IDb", AF.Identity, 0.0, -2048.0)

    def late_rows():
        for f, s in ((R_N, "nBH"), (R_N + 1, "nBL"), (R_ITM, L("LH", O_ITM)), (R_ITM + 1, L("LL", O_ITM)), (R_ONE, "nzB"),
                     (R_BIT, L("LH", O_BIT))):
            row("sp", "late", "W", f, s)

    def before_verdict0():
        iota(("ZZ", ZM * ZW, ZL * ZW), [[0, (ZL - ZM) * ZW]])
        extI("p1", "W", "sb0")
        extI("p0", "W", "i2b", 0, NW, True, False)
        aconsts1()
        gather("act", "X", ("W", 0, NW), "par16", 0, NW)
        scatter(0, 800)
        cp("side16", P("p1"))
        ts(("thb", 0, 1), ("thI", 0, 1), -1.0, MUL, 0.5, ADD)
        ts("bitI", P("p1"), 0.0, LT)
        scatter(800, NW)
        extI("p2", "X", "itm")
        x_rows(0, L("LH", O_PAR), L("LL", O_PAR))
        gather("act", "SG", ("W", 0, NW), "side16", 0, H)

    def after_verdict0():
        make_z("pd", "kp")
        asel("npre", T.npre[:], "n2560", T.n2560[:], [[-1, NC]], GE_, 0.0, UA // 16 - 1, 0)
        make_z("r", "drop", "js", "jzp")
        gather("act", "SG", ("W", 0, NW), "side16", H, NW)
        act("sA0", P("p1"), AF.Relu)
        act("nbI", "bitI", AF.Identity, 1.0, -1.0)
        mm(P("p3"), "M2", "bitI", True, False)
        mm(P("p6"), "NId", L("LH", O_SIDE), True, False)
        mm(P("p6"), "NId", L("LL", O_SIDE), False, False)
        extI("p0", "SG", "sg0", 0, H, False, False)
        extB("p6", "SG", "side", 0, 8, False, False)
        extI("p0", "SG", "sg0", H, NW, False, True)
        extI("p3", "GE", "a0", 0, NW, False, True)
        cp("ip16", P("p2"))
        gather("act", "Ua", ("Ua", 0, NW), "par16", 0, 480, shift=NW)
        act("kaT", P("p0"), AF.Identity, -4096.0)
        gather("act", "Ua", ("Ua", 0, NW), "par16", 480, UA, shift=NW)
        add_own(0, "Ua")
        iota(("ZZ", ZL * ZW, len(ZS) * ZW), [[0, (len(ZS) - ZL) * ZW]])
        make_z("jzm", "jn", "sb1", "i2bn", "sg1", "a1")
        extI("p7", "GE", "n")
        extB("p6", "SG", "side", 8, 16, False, True)

    def late_lists0():
        tt("bpI", P("p7"), "bitI", MUL)
        tt("t3", P("p7"), "nI", SUB)
        mm(P("p4"), "IDf", "sA0", True, False)
        mm(P("p4"), "IDf", "bpI", False, True)
        act("DH", "t3", AF.Copy)

    def late_lists1():
        cp("pt16", P("p4"))
        tt("DL", "t3", "DH", SUB)

    def w_half(bank, win, z, h):
        return lambda: extI(bank, win, z, HALF[h][0], HALF[h][1])

    spare1 = [lambda: cp("pJ", "pB"),
              lambda: ts("pK", "pJ", 0xFF0, AND),
              lambda: cp("qH", "pK"),
              lambda: tt("qL", "pJ", "pK", SUB),
              lambda: cp("par16", P("p2")),
              lambda: tt("t1", "predI", "bpI", SUB)]

    def par_rows():
        row("sp", "pr1", "W", R_PAR, "qH")
        row("sp", "pr1", "W", R_PAR + 1, "qL")

    def before_verdict1():
        act("sA1", P("p3"), AF.Relu, -4096.0)
        gather("act", "X", ("W", 0, NW), "par16", 0, NW)
        mm(P("p1"), "IDf", "t1", True, False)
        mm(P("p1"), "IDf", "sA1", False, True)
        extI("p2", "W", "i2bn", 0, NW, True, False)
        x_rows(1, "pH", "pL")
        gather("dve", "Uc", ("Uc", 0, NW), "par16", 960, UA, shift=NW)
        cp("pt16", P("p1"))
        gather("dve", "Uc", ("Uc", 0, NW), "par16", 640, 960, shift=NW)
        gather("dve", "C", ("W", 0, NW), "pt16", 0, H)
        gather("dve", "C", ("W", 0, NW), "pt16", H, NW)

    def after_verdict1():
        gather("act", "Uc", ("Uc", 0, NW), "par16", 0, 640, shift=NW)
        add_own(1, "Uc")
        mm(P("p3"), "M2", "nbI", True, False)
        for h, (a, b) in enumerate(HALF):
            extI("p2", "C", "sg1", a, b, False, h == 1)
            extI("p3", "C", "a1", a, b, False, h == 1)
        extI("p7", "X", "itm")
        act("kaT", P("p2"), AF.Identity, 1024.0 - 2 * BIG)
        tt("t2", P("p3"), "kaT", MIN)
        ts("ka16", "t2", 2048.0 + 2 * BIG, ADD, 1024.0, MIN)
        cp("ip16", P("p7"))

    def splice_merge(t, U, U1, U2):
        kw = ("KW%d" % t, 0, NI + 1)
        arr = [verdicts_in(t)]
        bank = ["p0", "p1", "p3"]

        def cvt(lst, q):
            a, b = PART[q]
            cp((lst, a // 16, b // 16), P(bank[q], (b - a) // 16))

        def drop(h):
            extI("p2", "KA", "drop", HALF[h][0], HALF[h][1], False, False)

        def verdicts(a, b):
            gather("dve", "A", kw, "ip16", a, b, "X", MUL, ext=arr)
        mm(P("p5"), "IDf", "npre", True, False)
        if t == 0:
            verdicts(0, FIRST)
            tt("t2", P("p3"), "kaT", MIN)
            verdicts(FIRST, FIRST + 160)
            ts("ka16", "t2", 6144.0, ADD, 1024.0, MIN)
        gather("act", "KA", kw, "ka16", 0, H, ext=arr)
        for q, (a, b) in enumerate(PART):
            if q == 2:
                verdicts(a, a + 384)
                cvt("j1", 0)
                if t == 0:
                    late_lists1()
            verdicts(FIRST + 160 if q == t == 0 else a + 384 * (q == 2), b)
            extI(bank[q], "A", "r", a, b, o=0)
            if q == 0:
                if t == 0:
                    late_lists0()
                gather("act", "KA", kw, "ka16", H, NW)
                mm(P("p2"), "IDf", "sA%d" % t, True, False)
            if q == 1:
                extI("p5", "A", "kp", 0, UA, False, False)
        chain = [("B", "A", "j1", "j2"), ("A", "B", "j2", "j4l"), ("B", "A", "j4l", None)]
        for lv, (o, win, lst, nxt) in enumerate(chain):
            for q, (a, b) in enumerate(PART):
                m = a + SPLIT[q]
                gather("act", o, win, lst, a, m)
                if q != 1:
                    gather("dve", o, win, lst, m, m + 192)
                    m += 192
                    if q == 0:
                        cvt(lst, 1)
                    elif nxt:
                        cvt(nxt, 0)
                gather("dve", o, win, lst, m, b)
                if q == 0:
                    cvt(lst, 2)
                if q == 1 and lv == 1:
                    cp("pe16", P("p5"))
                if q == 0 and lv == 2:
                    drop(1)
                if nxt:
                    extI(bank[q], o, "r", a, b, o=0)
                else:
                    extI("p5", o, "js", a, b)
                if lv == 0 and q == 0:
                    extI("p5", "A", "pd", UA, NW, False, True)
                if q == 0 and lv == 1:
                    drop(0)
        row("sp", "rp%d" % t, "A", 0, "nIH")
        row("sp", "rp%d" % t, "A", 1, "nIL")
        for h, (a, m, b) in enumerate(((0, 768, 1600), (1600, 2080, NW))):
            gather("act", "C", "B", "pt16", a, m)
            gather("dve", "C", "B", "pt16", m, b)
            extI("p2", "C", "jzp", a, b, False, h == 1)
            if h == 0:
                act("t1", P("p5"), AF.Identity, 0.0, -4096.0)
                mm(P("p2"), "IDf", "t1", False, False)
        def spliced(j):
            a, b = PIECE[j]
            if a < UA:
                gather("act", U1, (U, 0, NW + UA), "pe16", a, b)
            else:
                gather("dve", U1, (U, 0, NW), "pe16", a, b, U, ADD, shift1=NW)
            return lambda: dma("sp", "ud%d_%d" % (t, j), T.Ud[:, a:b], T[U1][:, a:b], [(U1, a, b)], [("Ud", a, b)])
        spliced(2)
        spliced(0)
        cp("p816", P("p5"))
        cp(("Ud",) + PIECE[2], (U1,) + PIECE[2])
        ts("mI", P("p2"), 0.0, EQ)
        ts("se16", P("p2"), float(NW), MIN, 0.0, MAX)
        tt("dH", "mI", "DH", MUL)
        row("sp", "rp%d" % t, "A", 2, "dH")
        tt("dL", "mI", "DL", MUL)
        row("sp", "rp%d" % t, "A", 3, "dL")
        if t == 0:
            act("SH", P("p6"), AF.Copy)
        copy1 = spliced(1)
        spliced(3)()
        copy1()
        act(("Ud",) + PIECE[0], (U1,) + PIECE[0], AF.Copy)
        if t == 0:
            tt("SL", P("p6"), "SH", SUB)
            act("predI", P("p7"))
            extB("p3", "KA", "drop", 0, 16, True, False)
            extB("p3", "B", "jzm", 0, 16, False, False)
            extB("p3", "C", "jzp", 0, 16, False, True)
        def finish(j):
            a, b = PIECE[LAST[j]]
            if t == 0:
                ge4(U2, a, b, j == 0, last=j == 3)
            else:
                ts(("Y", a, b), (U2, a, b), 15.0, MIN)
                dma("sp", "yc%d" % j, T.yc[:, a:b], T.Y[:, a:b], [("Y", a, b)], [])
        for j, (a, b) in enumerate(TAIL):
            gather("act", "SG", "A", "p816", a, b)
            gather("dve", U2, (U1, 0, NW + 1), "se16", PIECE[LAST[j]][0], PIECE[LAST[j]][1], "Ud", ADD)
            extB("p4", "SG", "jn", a // NC, b // NC, a == 0, b == NW)
            if t == 0 and j == 2:
                ts("mB", P("p3"), 0.0, EQ)
            if j and not (t == 0 and j == 3):
                finish(j - 1)
            if t == 0 and j == 2:
                for f, o, d in ((R_DS, "sH", "SH"), (R_DS + 1, "sL", "SL")):
                    tt(o, "mB", d, MUL)
                    row("sp", "sd1", "W", f, o)
                add_up("p4", [("NId", x) for x in (L("LH", O_SIDE), L("LL", O_SIDE), "sH", "sL")], False, False)
                finish(2)
        finish(3)
        if t == 0:
            act(("Y", UA, NW), (U2, UA, NW), AF.Relu, 15.0, -1.0)
            act("eH", P("p4"), AF.Copy)
            act(("Y", 9 * NC, UA), (U2, 9 * NC, UA), AF.Relu, 15.0, -1.0)
        else:
            act("pB", P("p4"))
            dma("act", "yp0", T.yp[:], T.pB[:], ["pB"], [])

    prep(0, "Ua")
    walks(0, [w_half("p3", "W", "par", 0), w_half("p3", "W", "par", 1), lambda: extI("p2", "W", "side"), nop],
          [aconsts0, selectors], spare0, late_rows)
    before_verdict0()
    verdict(0)
    after_verdict0()
    splice_merge(0, "Ua", "Ub", "Uc")
    prep(1, "Uc")
    extI("p2", "SG", "jn", 0, H)
    walks(1, [w_half("p2", "SG", "jn", 1), w_half("p3", "W", "sb1", 0), w_half("p3", "W", "sb1", 1), nop], [nop, nop],
          spare1, par_rows)
    before_verdict1()
    verdict(1)
    after_verdict1()
    splice_merge(1, "Uc", "Ub", "Ua")

    total = {}
    for o in ops:
        if o["grp"]:
            total["d_" + o["grp"]] = total.get("d_" + o["grp"], 0) + 16
    count = {}
    for o in ops:
        if o["grp"]:
            o["done"] = ("d_" + o["grp"], total["d_" + o["grp"]])
        elif o["inc"]:
            s = "e_" + o["e"]
            count[s] = count.get(s, 0) + 1
            o["done"] = (s, count[s])
        else:
            o["done"] = None
    total.update(count)

    def meet(a, b):
        return a[1] < b[2] and b[1] < a[2] and (a[3] is None or b[3] is None or a[3] == b[3])

    seen = {}
    waited = {}
    for o in ops:
        need = {}
        for s, v in o["ext"]:
            need[s] = v
        acc_ = [(x, False) for x in o["r"]] + [(x, True) for x in o["w"]]
        for x, wr in acc_:
            psum = SCRATCH[x[0]][0] == "psum"
            for y, ywr, q in seen.get(x[0], []):
                if q["done"] is None or (q["grp"] and q["grp"] == o["grp"]):
                    continue
                same = q["e"] == o["e"] and not q["grp"] and not o["grp"]
                if same and o["e"] == "pe":
                    continue
                if (psum and not same) or ((wr or ywr) and meet(x, y)):
                    s, v = q["done"]
                    need[s] = max(need.get(s, 0), v)
        for x, wr in acc_:
            seen.setdefault(x[0], []).append((x, wr, o))
        for s in sorted(need):
            if waited.get((o["e"], s), 0) < need[s]:
                Q[o["e"]].wait_ge(T.sem[s], need[s])
                waited[(o["e"], s)] = need[s]
        ins = o["fn"]()
        if o["done"]:
            ins.then_inc(T.sem[o["done"][0]], 16 if o["grp"] else 1)
    total["sent"] = sent[0]
    for s in sorted(total):
        g.wait_ge(T.sem[s], total[s])
